import numpy as np, ml_dtypes
CORES = [48,51,52,55]
N = 4
import mx_ref
BF = ml_dtypes.bfloat16
def gentries(a):
    return np.ascontiguousarray(a.reshape(8, 16, -1).transpose(0, 2, 1)).reshape(8, -1)
def gtable(e):
    e = np.asarray(e); return np.ascontiguousarray(e.reshape(8, -1, 16).transpose(0, 2, 1)).reshape(128, -1).astype(np.int32)
def gcols(t, e):
    v = np.concatenate([t.reshape(8, 16, -1, 4), np.zeros((8, 16, 1, 4), BF)], axis=2)
    return np.ascontiguousarray(np.stack([v[g][:, e[g]] for g in range(8)])).reshape(128, -1)
def tile(rs):
    return np.stack(rs, axis=2).reshape(128, -1).astype(BF)
def cut(t, i, w=512):
    return t[:, w * i:w * i + w]
def pick(q, e):
    c = np.concatenate([q[0].reshape(128, -1, 4), np.zeros((128, 1, 4), np.uint8)], axis=1); s = np.concatenate([q[1], np.ones((16, 1), np.uint8)], axis=1)
    return (np.ascontiguousarray(c[:, e].reshape(128, -1)), np.ascontiguousarray(s[:, e]))
def join(*qs):
    return (np.concatenate([q[0] for q in qs], axis=1), np.concatenate([q[1] for q in qs], axis=1))
def put(q, e, v):
    c, s = q[0].reshape(128, -1, 4).copy(), q[1].copy(); c[:, e] = v[0].reshape(128, -1, 4); s[:, e] = v[1]
    return (c.reshape(128, -1), s)
def pk(c, s):
    return (np.ascontiguousarray(c), mx_ref.live(s))
def emit(q):
    return q[0], q[1]
def packed(v, rng):
    q = [mx_ref.quantize(np.ascontiguousarray(v[r])) for r in range(N)]
    return np.stack([a for a, b in q]), np.stack([mx_ref.plane(b, rng) for a, b in q])
def values_of_codes():
    e, c = np.zeros((128, 128, 4), np.float32), np.zeros((128, 2, 4), np.uint8)
    e[np.arange(128), np.arange(128), 0] = 1
    c[:127, :, 0] = np.arange(256).reshape(2, 128).T[:127]
    return mx_ref.matmul(mx_ref.quantize(e.reshape(128, 512).astype(BF)), (c.reshape(128, 8), np.full((16, 2), 127, np.uint8))).T.reshape(-1).astype(np.float64)
CODE_VALUE, SCALE_VALUE = values_of_codes(), 2.0 ** (np.arange(256) - 127.0)
def decode(q):
    return (CODE_VALUE[q[0]].reshape(16, 8, -1, 4) * SCALE_VALUE[q[1]][:, None, :, None] + 0.0).reshape(128, -1).astype(np.float32)
def f(rng, *shape):
    return mx_ref.flush((rng.standard_normal(shape, dtype=np.float32) * np.exp2(rng.integers(-2, 3, shape[:-1] + (1,)))).astype(BF))
def wide(rng, *shape, cols=0):
    v = rng.standard_normal(shape, dtype=np.float32) * np.exp2(rng.integers(-12, 13, shape)).astype(np.float32)
    if cols: v *= np.repeat(np.exp2(rng.integers(-cols, cols + 1, shape[:-2] + (1, shape[-1] // 4))) * (rng.random(shape[:-2] + (1, shape[-1] // 4)) > 0.0625), 4, axis=-1).astype(np.float32)
    return mx_ref.flush(v.astype(BF))
C, S = 384, 48
def stored(j):
    e = j.reshape(2, 8, N, C).transpose(2, 1, 0, 3).reshape(N, 8, 2 * C)
    return np.stack([gtable(e[r]) for r in range(N)])
def both(a):
    return np.stack([gentries(a[r]) for r in range(N)]).reshape(N, 8, 2, C).transpose(2, 1, 0, 3).reshape(2, 8, N * C)
def seats(rng):
    p = rng.permutation(N)
    return p, [np.stack([rng.permutation(C) for r in range(N)]) for h in range(3)]
def place(rng, s, u, seat=None, bits=False):
    p, w = seat or seats(rng)
    n = []
    for h, o in zip((np.zeros(C, int), np.array(s), np.array(u)), w):
        b = p[np.arange(N)[:, None] ^ h if bits else (np.arange(N)[:, None] + h) % N]
        n.append(C * b + o[b, np.arange(C)])
    j, k = np.zeros(N * C, int), np.zeros(N * C, int)
    j[n[0]], k[n[0]] = n[1], n[2]
    return j, k
def roam(rng):
    s, u = [0] * C, [0] * C
    n = [[0] * N for k in range(3)]
    n[0][0] = n[1][0] = n[2][0] = C
    def add(a, b, w):
        n[0][a] += w
        n[1][b] += w
        n[2][(b - a) % N] += w
    for t, a, b in zip(rng.integers(0, C, 6 * C).tolist(), rng.integers(0, N, 6 * C).tolist(), rng.integers(0, N, 6 * C).tolist()):
        add(s[t], u[t], -1)
        add(a, b, 1)
        if max(max(m[1:]) for m in n) <= S:
            s[t], u[t] = a, b
        else:
            add(a, b, -1)
            add(s[t], u[t], 1)
    return s, u
def brim(rng, kind):
    s = np.zeros(C, int)
    m = np.repeat(1 + rng.permutation(N - 1), S)[:C]
    s[:len(m)] = m
    z = np.zeros(C, int)
    return ((s, s), (s, z), (z, s), (z, z))[kind]
def apart(n):
    x = np.array({4: [1, 2, 3], 8: [1, 2, 4, 3, 6, 7, 5]}[N])
    t = np.arange(C)
    return [np.where(t < 144, x[(t + h) % (N - 1)], 0) for h in ((0, 1), (3, 2))[n]]
def lists_of(rng, steps):
    e = [[place(rng, *steps[n][g]) for g in range(8)] for n in range(2)]
    return np.array([[p[0] for p in h] for h in e]), np.array([[p[1] for p in h] for h in e])
def big(v, k, low=-12):
    v = v.astype(np.float32) * np.float32(k)
    v[np.abs(v) < np.float32(2.0 ** low)] = 0
    return v.astype(BF)
def weights(rng, k, low=-20):
    c, p = packed(big(f(rng, N, 128, 2048), k, low), rng)
    return {"wc": c, "ws": p}
def numbers_of(rng):
    return {"xb": big(f(rng, N, 128, 4 * C), 1), "xc": big(f(rng, N, 128, 4 * C), 1), "v": np.array(f(rng, N, 128, 512))}
def with_lists(d, jk):
    return {**d, "jb": stored(jk[0]), "kc": stored(jk[1])}
def setup_inputs(rng):
    d = {**numbers_of(rng), **weights(rng, 0.25)}
    return with_lists(d, lists_of(rng, [[roam(rng) for g in range(8)] for n in range(2)]))
def setup_inputs_full(rng):
    d = {**numbers_of(rng), **weights(rng, 0.25)}
    return with_lists(d, lists_of(rng, [[brim(rng, k % 4) for k in rng.permutation(8)] for n in range(2)]))
def setup_inputs_shared(rng):
    d = {**numbers_of(rng), **weights(rng, 0.25)}
    s, u = np.zeros(C, int), np.zeros(C, int)
    s[:3 * S] = np.repeat([1, 2, N - 1], S)
    u[:2 * S] = np.repeat([3, 1], S)
    e = []
    for far in rng.permutation(8) % 2:
        p, w = seats(rng)
        if far:
            e.append([place(rng, *apart(n), (p, [np.roll(o, n * 144, axis=1) for o in w]), True) for n in range(2)])
        else:
            e.append([place(rng, s, u, (p, w)), place(rng, s, u, (p, [np.roll(o, 2 * S, axis=1) for o in w]))])
    return with_lists(d, np.array(e).transpose(2, 1, 0, 3))
def setup_inputs_twins(rng):
    d = {**numbers_of(rng), **weights(rng, 0.25)}
    e = [roam(rng) for g in range(8)]
    j, k = lists_of(rng, [e, e])
    g = (rng.permutation(8) % 2 == 0)[:, None]
    j[1], k[1] = np.where(g, j[0], k[0]), np.where(g, k[0], j[0])
    return with_lists(d, (j, k))
def setup_inputs_gaps(rng):
    d = setup_inputs(rng)
    e = rng.permutation(N)
    d["xb"][e[0]] = 0
    d["xc"][e[1]] = np.tile(d["xc"][e[1]][:, :4], (1, C))
    g = int(rng.integers(8))
    d["xc"][e[2], 16 * g:16 * g + 16] = 0
    return d
def setup_inputs_spread(rng):
    d = {**setup_inputs(rng), **weights(rng, 2.0 ** -8, -24)}
    for n in ("xb", "xc"): d[n] = big(wide(rng, N, 128, 4 * C, cols=3), 2.0 ** -6)
    return d
def check_inputs(d):
    b = []
    for k in ("xb", "xc", "v"):
        a = np.abs(d[k].astype(np.float32))
        if not (np.isfinite(a).all() and ((a == 0) | (a >= 2.0 ** -30) & (a <= 2.0 ** 30)).all()): b.append("a value of " + k)
    e = {k: both(d[k]) for k in ("jb", "kc")}
    for k in ("jb", "kc"):
        if (np.sort(e[k], axis=2) != np.arange(N * C)).any(): b.append("a number that isn't there exactly once in a half and group of " + k)
    if any(((e[k] < 0) | (e[k] >= N * C)).any() for k in e): return b
    own = np.arange(N * C) // C
    over = set()
    for n in range(2):
        for g in range(8):
            j, k = e["jb"][n, g] // C, e["kc"][n, g] // C
            for name, p, q in (("A and B", own, j), ("A and C", own, k), ("B and C", j, k)):
                c = np.bincount(N * p + q, minlength=N * N).reshape(N, N)
                np.fill_diagonal(c, 0)
                if c.max() > S: over.add("too many nonzeros between two ranks: " + name)
    return b + sorted(over)
def held(q):
    return decode(join(*q)).astype(BF)
def pairs(p, q, e, h):
    a, b = [gcols(p, e[n]).astype(np.float32) * gcols(q, h[n]).astype(np.float32) for n in range(2)]
    return (a + b).astype(BF)
def layer(lay, m):
    o = []
    for r in range(N):
        q = mx_ref.quantize(np.ascontiguousarray(cut(m, r, 4 * C)))
        o.append(mx_ref.quantize(tile([mx_ref.matmul(pick(lay[r], np.arange(128 * b, 128 * b + 128)), q) * np.float32(0.03125) for b in range(4)])))
    return o
def reference(xb, xc, v, wc, ws, jb, kc):
    lay = [pk(wc[r], ws[r]) for r in range(N)]
    j, k = both(jb), both(kc)
    oldb = held([mx_ref.quantize(xb[r]) for r in range(N)])
    oldc = held([mx_ref.quantize(xc[r]) for r in range(N)])
    qa = layer(lay, pairs(oldb, oldc, j, k))
    newa = held(qa)
    i = np.argsort(j, axis=2)
    qb = layer(lay, pairs(newa, oldc, i, np.take_along_axis(k, i, axis=2)))
    newb = held(qb)
    i = np.argsort(k, axis=2)
    qc = layer(lay, pairs(newa, newb, i, np.take_along_axis(j, i, axis=2)))
    y = np.zeros((N, 128, 3 * C), np.float32)
    oc, osc = np.zeros((N, 128, 12 * C), np.uint8), np.zeros((N, 16, 3 * C), np.uint8)
    for r in range(N):
        q = join(qa[r], qb[r], qc[r])
        y[r] = mx_ref.matmul(mx_ref.quantize(v[r]), q)
        oc[r], osc[r] = emit(q)
    return {"y": y, "oc": oc, "osc": osc}

@@ -1,0 +1,504 @@
+from concourse.bass import DstId, RemoteDMATransfer
+from concourse.mybir import dt, AluOpType, AxisListType, ActivationFunctionType
+
+N = 4
+C = 384
+S = 48
+SL = 2 * S
+R = (N - 1) * SL
+CH = ((0, 256), (256, 128))
+LW = 2 * C // 16
+SW = R // 16
+ROW = SW + LW
+WN = R + C
+W3 = 2 * C + R
+EMPTY = -4096.0
+
+X4, U8, BF, F32, I32, U16 = "float8_e4m3fn_x4", "uint8", "bfloat16", "float32", "int32", "uint16"
+SCRATCH = {"ps": ("psum", [128, 4096], F32), "kD": ("sbuf", [128, 3, 32], F32)}
+
+
+def _sb(dtype, **kw):
+    for name, n in kw.items():
+        SCRATCH[name] = ("sbuf", [128, n], dtype)
+
+
+_PAIRS = dict(W=512, V=128, E=512, Ee=512, Eo=512, C0=N * C, B0=WN, A=WN, B1=WN, C1=C, M1=C, M2=C, M3=C,
+              sB0=R, sA=R, sB1=R, F=2 * R, LF=2 * R)
+_sb(X4, **{"q" + k: n for k, n in _PAIRS.items()})
+_sb(U8, **{"s" + k: n for k, n in _PAIRS.items()})
+_sb(BF, txb=4 * C, pxb=4 * C, txc=4 * C, tv=512, tE=516, tEe=516, tEo=516, one=8 * ROW, wC=4 * N * C, wB=4 * WN, wA=4 * WN, w3=4 * W3,
+    gC=8 * C, gA=8 * C, g3=4 * C, p1=4 * C, p2=4 * C, n1=512, n2=512, fA=4 * R, m1=4 * C, m2=4 * C, m3=4 * C,
+    tA=4 * C, tB=4 * C, tC=4 * C, cB0=4 * R, cA=4 * R, cB1=4 * R)
+_sb(F32, yt=3 * C, msk=8, mskD=2, r24=160, r16=160, row1=16 * ROW, row3=16 * ROW, val3=2 * C, tab=N * C, pos1=R, pos3=R, val2=R,
+    kM=192, kS=160, kY=192, kZ=160, kX=160, kU=192, kV=192, kA=2 * LW, kT=96,
+    lJ=ROW, lK=ROW, lI=ROW, rJ=SW, rK=SW, lP=ROW, lQ=ROW, mJ=ROW, mK=ROW, rK3=SW, mP=ROW, dupe=16 * ROW, dupo=16 * ROW,
+    fE=ROW, fO=ROW, hE=SW, u1=2 * LW)
+_sb(I32, jw=LW, kw=LW, val1=2 * C, cD=4 * SW, cS=4, kO=LW, kG=LW, kL=2 * LW, kR=LW, hL=5 * SW)
+_sb(U16, oS=4, oT=LW, oH=SW, oK=SW, oK1=LW, oP1=LW, oP2=LW, oK2=LW, oP3=LW, oB0=SW, oA=4 * SW, oB1=4 * SW, oF=2 * SW)
+
+SEMAPHORES = (["cv", "cs", "ct", "cg", "sent", "aJ", "aK", "aK3", "aB0", "aA", "aB1", "aF"]
+              + ["aC%d" % k for k in range(N)] + ["d%d" % k for k in range(48)])
+
+ADD, SUB, MUL, MAX, MIN = AluOpType.add, AluOpType.subtract, AluOpType.mult, AluOpType.max, AluOpType.min
+EQ, AND, SHR = AluOpType.is_equal, AluOpType.bitwise_and, AluOpType.arith_shift_right
+COPY, IDENT = ActivationFunctionType.Copy, ActivationFunctionType.Identity
+
+
+def rank_program(g, core, T, topo):
+    rank = T.rank_of(core)
+    if rank is None:
+        return
+    lo = C * rank
+    peers = [(rank + 1 + t) % N for t in range(N - 1)]
+    pcore = [T.cores[o] for o in peers]
+    Q = {"v": g.vector, "s": g.scalar, "t": g.tensor, "g": g, "y": g.sync}
+    total, waited, writer, readers, free, spare = {}, {}, {}, {}, [0, 0], []
+
+    def need(e, toks):
+        top = {}
+        for s, v in toks:
+            top[s] = max(top.get(s, 0), v)
+        for s, v in top.items():
+            if waited.get((e, s), 0) < v:
+                Q[e].wait_ge(T.sem[s], v)
+                waited[(e, s)] = v
+
+    def deps(e, reads, writes, more=False):
+        toks = []
+        for k in reads:
+            toks.append(writer[k])
+            if k.startswith("ps"):
+                toks += [t for t in readers.get(k, []) if t[0] != "c" + e]
+        for k in writes:
+            if k in writer and not more:
+                toks.append(writer[k])
+            toks += readers.get(k, [])
+        need(e, toks)
+
+    def mark(tok, reads, writes):
+        for k in reads:
+            readers.setdefault(k, []).append(tok)
+        for k in writes:
+            writer[k], readers[k] = tok, []
+
+    def op(e, call, reads, writes, more=False):
+        if e == "v" and spare and not free[1] and any(writer[k] == ("cv", total["cv"]) for k in reads):
+            free[1] = 1
+            spare.pop(0)()
+            free[1] = 0
+        deps(e, reads, writes, more)
+        s = "c" + e
+        total[s] = total.get(s, 0) + 1
+        call().then_inc(T.sem[s], 1)
+        mark((s, total[s]), reads, writes)
+
+    def flush():
+        while spare:
+            spare.pop(0)()
+
+    def dma(e, moves, reads, writes, add=False):
+        deps(e, reads, writes)
+        s = "d%d" % free[0]
+        free[0] += 1
+        for out, src in moves:
+            (g.dma_start(out, src, accum_op=ADD) if add else Q[e].dma_start(out, src)).then_inc(T.sem[s], 16)
+        total[s] = 16 * len(moves)
+        mark((s, total[s]), reads, writes)
+
+    def remote(moves, sem, reads):
+        deps("g", reads, [])
+        ts_ = []
+        for ts, es, src, dst in moves:
+            ids = [DstId(rid=topo.addr(pcore[t])[0], pnc=topo.addr(pcore[t])[1]) for t in ts]
+            ts_.append(RemoteDMATransfer(dst_ids=ids, dma_engine_mask=sum(1 << x for x in es), remote_sem=T.sem[sem],
+                                         srcs=[src], dsts=[dst] * len(ts)))
+            total["sent"] = total.get("sent", 0) + len(es)
+        g.remote_dma_fused(ts_, local_sem=T.sem.sent)
+
+    def landed(sem, n, keys):
+        total[sem] = n
+        mark((sem, n), [], keys)
+
+    eng = [x for x in topo.engines(core, pcore[0]) if all(x in topo.engines(core, c) for c in pcore)]
+    ne = len(eng)
+    order = sorted(range(N - 1), key=lambda t: topo.die(pcore[t]) != topo.die(core))
+    qt = ne // 4
+    wide = dict(zip(order, (eng[:qt], eng[qt:2 * qt], eng[2 * qt:])))
+    thin = dict(zip(order, (eng[2 * qt:3 * qt], eng[3 * qt:], eng[:2 * qt])))
+
+    def share(src, dst):
+        r = T.cores.index(src)
+        ps = [T.cores[(r + 1 + t) % N] for t in range(N - 1)]
+        o = sorted(range(N - 1), key=lambda t: topo.die(ps[t]) != topo.die(src))
+        return 2 * qt if ps[o[-1]] == dst else qt
+
+    got = sum(share(c, core) for c in pcore)
+
+    def u8(ap):
+        return ap.bitcast(dt.uint8)
+
+    def send_list(src, dst, sem, reads, key):
+        w = SL // 16
+        remote([([t], wide[t], src[:, w * t:w * t + w], dst[:, w * (N - 2 - t):w * (N - 1 - t)]) for t in range(N - 1)], sem, reads)
+        landed(sem, got, [key])
+
+    def send_slots(src, dst, sem, reads, key):
+        at = [(t, SL * t, SL * (N - 2 - t)) for t in range(N - 1)]
+        remote([([t], wide[t], u8(T["q" + src][:, a:a + SL]), u8(T["q" + dst][:, b:b + SL])) for t, a, b in at], sem, reads)
+        remote([([t], thin[t], T["s" + src][:, a:a + SL], T["s" + dst][:, b:b + SL]) for t, a, b in at], sem, reads)
+        landed(sem, 2 * got, [key])
+
+    def ts(out, src, s1, s2, o0, o1, reads, writes):
+        if o1 is None:
+            op("v", lambda: g.vector.tensor_scalar(out, src, s1, None, o0), reads, writes)
+        else:
+            op("v", lambda: g.vector.tensor_scalar(out, src, s1, s2, o0, o1), reads, writes)
+
+    def tt(out, a, b, o, reads, writes):
+        op("v", lambda: g.vector.tensor_tensor(out, a, b, o), reads, writes)
+
+    def cp(e, out, src, reads, writes):
+        if e == "v":
+            op("v", lambda: g.vector.tensor_copy(out, src), reads, writes)
+        else:
+            op("s", lambda: g.scalar.activation(out, src, COPY), reads, writes)
+
+    def act(out, src, bias, scl, reads, writes):
+        op("s", lambda: g.scalar.activation(out, src, IDENT, bias=bias, scale=scl), reads, writes)
+
+    def fill(ap, v, writes):
+        op("v", lambda: g.vector.memset(ap, v), [], writes)
+
+    def quant(name, a, n, tile, reads, writes):
+        op("v", lambda: g.vector.quantize_mx(T["q" + name][:, a:a + n], T["s" + name][:, a:a + n], tile), reads, writes)
+
+    def mm(bank, w, wa, x, a, n, reads, start=True, stop=True):
+        op("t", lambda: g.tensor.matmul_mx(T.ps[:, 512 * bank:512 * bank + n], T["q" + w][:, wa:wa + 128], T["s" + w][:, wa:wa + 128],
+                                           T["q" + x][:, a:a + n], T["s" + x][:, a:a + n], start, stop),
+           reads, ["ps%d" % bank], more=not start)
+
+    def bank(k, n):
+        return T.ps[:, 512 * k:512 * k + n]
+
+    def unpack(b0, x, a, n, reads):
+        for b in range(4):
+            mm(b0 + b, "E", 128 * b, x, a, n, ["qE%d" % b] + reads)
+
+    def window(es, b0, win, width, a, n, key):
+        for b in range(4):
+            cp(es[b], win[:, width * b + a:width * b + a + n], bank(b0 + b, n), ["ps%d" % (b0 + b)], ["%s%d" % (key, b)])
+
+    def iota(ap, pattern, base, mult, writes, small=False, reads=()):
+        if small:
+            op("g", lambda: g.iota(ap, pattern, base, mult, allow_small_or_imprecise_dtypes=True), list(reads), writes)
+        else:
+            op("g", lambda: g.iota(ap, pattern, base, mult), list(reads), writes)
+
+    def own_columns(row, base, key, small):
+        iota(row[:, 0:256], [[1, 16], [16, 16]], base, 0, [key + "0"], small)
+        iota(row[:, 256:512], [[1, 16], [128 - C, 2], [16, 8]], base + 256, 0, [key + "1"], small)
+        iota(row[:, 512:768], [[1, 16], [16, 16]], base + 512 - C, 0, [key + "2"], small)
+
+    def rows(row, part, src, a=0):
+        return [(row[part:128:16, 256 * u:256 * u + 256], src[:, a + 16 * u:a + 16 * u + 16]) for u in range(3)]
+
+    def unit(name):
+        for b in range(4):
+            quant(name, 128 * b, 128, T["t" + name][:, 3 - b:515 - b], ["t" + name], ["q%s%d" % (name, b)])
+
+    def by_element(out, src, base, reads, key, bs=range(4)):
+        for t in bs:
+            ts(out[:, SW * t:SW * t + SW], src, 4.0, float(t - 4 * base), MUL, ADD, reads, ["%s%d" % (key, t)])
+
+    def compose(es, tile, src, off, name, reads):
+        for t in (0, 2, 1, 3):
+            cp(es[t], tile[:, t:4 * R:4], src[:, 0:4 * C].indirect(off[:, SW * t:SW * t + SW]), reads + ["o%s%d" % (name, t)], ["c%s%d" % (name, t)])
+
+    def post(tile, name, sem):
+        quant("s" + name, 0, R, tile[:], ["c%s%d" % (name, t) for t in range(4)], ["qs" + name])
+        send_slots("s" + name, name, sem, ["qs" + name], "q%sa" % name)
+
+    km = ["kM%d" % t for t in range(N)]
+    h = LW // 2
+
+    def sort_a(X, xk):
+        ts(T.kO[:], X, 1.0 / C, 0.5 / C - 0.5, MUL, ADD, [xk], ["kO"])
+        for n in range(2):
+            ts(T.kU[:, 3 * LW + h * n:3 * LW + h * n + h], X[:, h * n:h * n + h], float(R - lo + C * n), None, ADD, None, [xk], ["kU%d" % (6 + n)])
+        for t, o in enumerate(peers + [rank]):
+            ts(T.kM[:, LW * t:LW * t + LW], T.kO[:], float(o), None, EQ, None, ["kO"], ["kM%d" % t])
+        op("v", lambda: g.vector.tensor_tensor_scan(T.kS[:], T.r24[:], T.kM[:, 0:160], 0.0, MUL, ADD), km + ["r24"], ["kS"])
+
+    def sort_b():
+        op("v", lambda: g.vector.transpose(T.kY[:, 32:192], T.kS[:]), ["kS"], ["kY"])
+        op("v", lambda: g.vector.tensor_tensor_scan(T.kZ[:], T.kY[:, 31:191], T.r16[:], 0.0, ADD, MUL), ["kY", "kYpad", "r16"], ["kZ"])
+        op("v", lambda: g.vector.transpose(T.kX[:], T.kZ[:]), ["kZ"], ["kX"])
+
+    def sort_c():
+        for k in range(2 * (N - 1)):
+            ts(T.kU[:, h * k:h * k + h], T.kS[:, h * k:h * k + h], T.kX[:, h * k + h - 1:h * k + h], float(S * k - 1), ADD, ADD,
+               ["kS", "kX"], ["kU%d" % k])
+        tt(T.kV[:], T.kU[:], T.kM[:], MUL, km + ["kU%d" % k for k in range(8)], ["kV"])
+        tt(T.kA[:], T.kV[:, 0:2 * LW], T.kV[:, 2 * LW:], ADD, ["kV"], ["kA"])
+        tt(T.kG[:], T.kA[:, 0:LW], T.kA[:, LW:], ADD, ["kA"], ["kG"])
+        ts(T.kL[:, 0:LW], T.kG[:], 15, None, AND, None, ["kG"], ["kL0"])
+        ts(T.kL[:, LW:], T.kG[:], 4, None, SHR, None, ["kG"], ["kL1"])
+        ts(T.kR[:], T.kL[:, 0:LW], float(ROW), None, MUL, None, ["kL0"], ["kR"])
+        for k in range(2):
+            tt(T.kD[:, :, 16 * k:16 * k + 16], T.kR[:], T.kL[:, LW:], ADD, ["kR", "kL1"], ["kD%d" % k])
+        op("v", lambda: g.vector.transpose(T.kT[:], T.kD[:]), ["kD0", "kD1"], ["kT"])
+        cp("v", T.oT[:], T.kT[:].indirect(T.oS[:, 0:3]), ["kT", "oS"], ["oT"])
+
+    def place(X, xk):
+        L = [T.hL[:, SW * k:SW * k + SW] for k in range(5)]
+        tt(T.hE[:], X, T.cD[:, 2 * SW:3 * SW], ADD, [xk, "cC"], ["hE"])
+        tt(L[0], T.hE[:], T.cD[:, SW:2 * SW], MAX, ["hE", "cD"], ["hI"])
+        ts(L[1], L[0], 15, None, AND, None, ["hI"], ["hL0"])
+        ts(L[2], L[0], 4, None, SHR, None, ["hI"], ["hL1"])
+        ts(L[3], L[1], float(ROW), None, MUL, None, ["hL0"], ["hR"])
+        tt(L[4], L[3], L[2], ADD, ["hR", "hL1"], ["hT"])
+        cp("v", T.oH[:], L[4], ["hT"], ["oH"])
+
+    def layer(m, src, tile, c, b0, es, reads):
+        a, n = CH[c]
+        quant(m, a, n, src, reads, ["q%s%d" % (m, c)])
+        for b in range(4):
+            mm(b0 + b, "W", 128 * b, m, a, n, ["qW", "q%s%d" % (m, c)])
+        for b in range(4):
+            out, reads, writes = T[tile][:, 4 * a + b:4 * (a + n):4], ["ps%d" % (b0 + b)], ["%s%d%d" % (tile, c, b)]
+            if es[b] == "v":
+                ts(out, bank(b0 + b, n), 0.03125, None, MUL, None, reads, writes)
+            else:
+                act(out, bank(b0 + b, n), 0.0, 0.03125, reads, writes)
+
+    def whole(tile):
+        return ["%s%d%d" % (tile, c, b) for c in range(2) for b in range(4)]
+
+    def listed(win, width, b, off, n, c):
+        a, k = CH[c]
+        return win[:, width * b:width * b + width].indirect(off[:, h * n + a // 16:h * n + (a + k) // 16])
+
+    def products(m, win, width, wkeys, off, okey, gt, gkey, c):
+        a, k = CH[c]
+        for b in range(4):
+            for n in range(2):
+                f = 2 * C * b + C * n + a
+                tt(T["mp"[n] + m][:, 4 * a + b:4 * (a + k):4], listed(win, width, b, off, n, c), gt[:, f:f + k], MUL,
+                   [x % b for x in wkeys] + [okey, "%s%d%d%d" % (gkey, b, n, c)], ["x%s%d%d%d" % (m, b, n, c)])
+
+    def parts(m, c):
+        return ["x%s%d%d%d" % (m, b, n, c) for b in range(4) for n in range(2)]
+
+    def mode(m, win, width, wkeys, off, okey, gt, gkey, tile, between, es):
+        e = 4 * CH[1][0]
+        products(m, win, width, wkeys, off, okey, gt, gkey, 0)
+        dma("g", [(T["m" + m][:, 0:e], T["p" + m][:, 0:e])], parts(m, 0), ["y" + m], add=True)
+        between()
+        products(m, win, width, wkeys, off, okey, gt, gkey, 1)
+        if m == "2":
+            layer("M" + m, T["m" + m][:, 0:e], tile, 0, 0, es[0], ["y" + m])
+        tt(T["n" + m][:], T["m" + m][:, e:], T["p" + m][:, e:], ADD, parts(m, 1), ["z" + m])
+        layer("M" + m, T["n" + m][:], tile, 1, 4, es[1], ["z" + m])
+        if m == "1":
+            layer("M" + m, T["m" + m][:, 0:e], tile, 0, 0, es[0], ["y" + m])
+
+    def store(f, name, a, key, es):
+        dma(es[0], [(T.oc[:, 4 * C * f:4 * C * (f + 1)], u8(T["q" + name][:, a:a + C]))], key, [])
+        dma(es[1], [(T.osc[4 * k:4 * k + 4, C * f:C * (f + 1)], T["s" + name][32 * k:32 * k + 4, a:a + C]) for k in range(4)], key, [])
+
+    dma("y", [(T.jw[:], T.jb[:])], [], ["jw"])
+    dma("y", [(T.txc[:], T.xc[:])], [], ["txc"])
+    dma("s", [(T.kw[:], T.kc[:])], [], ["kw"])
+    fill(T.one[:], 1.0, ["one"])
+    op("g", lambda: g.affine_select(T.tE[:], T.one[:, 0:516], [[-1, 516]], EQ, 0.0, 3, 4), ["one"], ["tE"])
+    own_columns(T.val1, R, "c1", False)
+    dma("y", [(T.txb[:], T.xb[:])], [], ["txb"])
+    dma("y", rows(T.val1, 1, T.jb) + rows(T.val1, 8, T.kc), ["c10", "c11", "c12"], ["val1"])
+    fill(T.r24[:], 1.0, ["r24"])
+    fill(T.r16[:], 1.0, ["r16"])
+    fill(T.msk[:, 2:3], 0.0, ["msk2"])
+    fill(T.kY[:, 0:32], 0.0, ["kYpad"])
+    fill(T.r24[:, 0:160:h], 0.0, ["r24"])
+    fill(T.r16[:, 0:160:16], 0.0, ["r16"])
+    for k in range(4):
+        fill(T.msk[32 * k:32 * k + 16, 2:3], 1.0, ["msk2"] if k in (0, 3) else [])
+    unit("E")
+    for row in ("row1", "row3"):
+        for k in range(2):
+            act(T[row][:, 8 * ROW * k:8 * ROW * (k + 1)], T.one[:], EMPTY, 0.0, ["one"], [row + "f%d" % k])
+    act(T.msk[:, 3:4], T.msk[:, 2:3], 1.0, -1.0, ["msk2"], ["msk3"])
+    act(T.tEe[:], T.tE[:], 0.0, T.msk[:, 2:3], ["tE", "msk2"], ["tEe"])
+    act(T.tEo[:], T.tE[:], 0.0, T.msk[:, 3:4], ["tE", "msk3"], ["tEo"])
+
+    sort_a(T.jw[:], "jw")
+    quant("C0", lo, C, T.txc[:], ["txc"], ["qC0%d" % rank])
+    every = list(range(N - 1))
+    remote([(every, eng, u8(T.qC0[:, lo:lo + C]), u8(T.qC0[:, lo:lo + C]))], "aC%d" % rank, ["qC0%d" % rank])
+    remote([(every, eng, T.sC0[:, lo:lo + C], T.sC0[:, lo:lo + C])], "aC%d" % rank, ["qC0%d" % rank])
+    for o in peers:
+        landed("aC%d" % o, 2 * ne, ["qC0%d" % o])
+    cS = ["cS%d" % k for k in range(4)]
+    for k in range(4):
+        iota(T.cS[32 * k:32 * k + 32, 0:3], [[32, 3]], 0, 1, [cS[k]], reads=["tE", "c10", "c11", "c12"])
+    unpack(0, "C0", lo, C, ["qC0%d" % rank])
+    window("ssss", 0, T.wC, N * C, lo, C, "wC%d" % rank)
+    for b in range(4):
+        cp("s", T.pxb[:, C * b:C * b + C], T.txb[:, b:4 * C:4], ["txb"], ["pxb%d" % b])
+    sort_b()
+    spare.extend([lambda: None, lambda: None, lambda: None,
+                  lambda: op("v", lambda: g.vector.tensor_reduce(T.msk[:, 4:5], T.tE[:, 35:516:64], AxisListType.X, ADD), ["tE"], ["msk4"]),
+                  lambda: cp("v", T.oK1[:], T.kw[:], ["kw"], ["oK1"]),
+                  lambda: cp("v", T.oS[:, 0:3], T.cS[:, 0:3], cS, ["oS"])])
+    sort_c()
+    cp("v", T.row1[:].indirect(T.oT[:]), T.val1[:], ["oT", "val1", "c10", "c11", "c12", "row1f0", "row1f1"], ["row1"])
+    near = [peers[t] for t in order]
+    dma("y", [(u8(T.qW[:]), T.wc[:]), (T.sW[:], T.ws[:])], ["qC0%d" % near[0]], ["qW"])
+    dma("y", [(T.lJ[:], T.row1[1:128:16, :])], ["row1"], ["lJ"])
+    dma("y", [(T.lK[:], T.row1[8:128:16, :])], ["row1"], ["lK"])
+    dma("y", [(T.lI[:], T.row1[0:128:16, :])], ["row1"], ["lI"])
+    dma("y", [(T.tv[:], T.v[:])], ["qC0%d" % near[2]], ["tv"])
+    iota(T.pos1[:], [[1, R]], 0, 0, ["pos10"], True, cS)
+    iota(T.tab[:], [[1, N * C]], 0, 0, ["tab0"], True)
+    iota(T.cD[:, 0:SW], [[16, SW]], 0, 1, ["cD0"])
+    iota(T.cD[:, 2 * SW:3 * SW], [[0, N - 1], [C, 2], [0, S // 16]], R - lo, 0, ["cC"])
+    send_list(T.lJ, T.rJ, "aJ", ["lJ"], "rJ")
+    send_list(T.lK, T.rK, "aK", ["lK"], "rK")
+    own_columns(T.val3, 0, "c3", True)
+    iota(T.pos3[:], [[SL, N - 1], [S - C, 2], [1, S]], 2 * C, 0, ["pos3"], True)
+
+    quant("B0", R, C, T.txb[:], ["txb"], ["qB0o"])
+    ts(T.cD[:, 3 * SW:3 * SW + 1], T.cD[:, 0:1], 112, None, AND, None, ["cD0"], ["cp1"])
+    ts(T.u1[:, 0:LW], T.kG[:], float(WN), float(C), AluOpType.is_ge, MUL, ["kG"], ["u1"])
+    cp("v", T.mskD[:, 0:1], T.cD[:, 3 * SW:3 * SW + 1], ["cp1"], ["msk0"])
+    tt(T.u1[:, LW:], T.kG[:], T.u1[:, 0:LW], SUB, ["kG", "u1"], ["u2"])
+    ts(T.cD[:, SW:2 * SW], T.cD[:, 0:SW], T.mskD[:, 0:1], None, SUB, None, ["cD0", "msk0"], ["cD"])
+    cp("v", T.oP1[:], T.u1[:, LW:], ["u2"], ["oP1"])
+    unpack(4, "C0", C * near[0], C, ["qC0%d" % near[0]])
+    window("ssss", 4, T.wC, N * C, C * near[0], C, "wC%d" % near[0])
+    unpack(0, "C0", C * near[1], C, ["qC0%d" % near[1]])
+    window("ssvv", 0, T.wC, N * C, C * near[1], C, "wC%d" % near[1])
+    unpack(4, "C0", C * near[2], C, ["qC0%d" % near[2]])
+    window("ssvv", 4, T.wC, N * C, C * near[2], C, "wC%d" % near[2])
+    unpack(0, "B0", R, C, ["qB0o"])
+    window("vvvs", 0, T.wB, WN, R, C, "wBo")
+    act(T.msk[:, 5:6], T.msk[:, 4:5], 1.0, -1.0, ["msk4"], ["msk5"])
+    act(T.tab[:], T.tab[:], 0.0, T.msk[:, 4:5], ["tab0", "msk4"], ["tab"])
+    act(T.pos1[:], T.pos1[:], 0.0, T.msk[:, 5:6], ["pos10", "msk5"], ["pos1"])
+
+    ts(T.oB0[:], T.rJ[:], float(lo), None, SUB, None, ["rJ"], ["oB0"])
+    for b in (0, 2, 1, 3):
+        cp("vvss"[b], T.cB0[:, b:4 * R:4], T.pxb[:, C * b:C * b + C].indirect(T.oB0[:]), ["pxb%d" % b, "oB0"], ["cB0%d" % b])
+    post(T.cB0, "B0", "aB0")
+    wCk = ["wC%d" % o + "%d" for o in range(N)]
+    for b in range(4):
+        cp("s", T.gC[:, 2 * C * b:2 * C * (b + 1)], T.wC[:, N * C * b:N * C * (b + 1)].indirect(T.oK1[:]),
+           [k % b for k in wCk] + ["oK1"], ["gC%d%d%d" % (b, n, c) for n in range(2) for c in range(2)])
+    spare.extend([lambda t=t: by_element(T.oA, T.lI[:, 0:SW], R, ["lI"], "oA", (t,)) for t in range(4)]
+                 + [lambda: cp("v", T.oK[:], T.rK[:], ["rK"], ["oK"])])
+    place(T.rJ[:], "rJ")
+    flush()
+    tt(T.val2[:], T.tab[:].indirect(T.oK[:]), T.pos1[:], ADD, ["tab", "oK", "pos1"], ["val2"])
+    cp("v", T.row1[:].indirect(T.oH[:]), T.val2[:], ["oH", "val2"], ["row1"])
+    dma("y", [(T.lQ[:], T.row1[8:128:16, :])], ["row1"], ["lQ"])
+    dma("y", [(T.lP[:], T.row1[0:128:16, :])], ["row1"], ["lP"])
+    dma("y", rows(T.val3, 0, T.lP, SW) + rows(T.val3, 8, T.lQ, SW), ["c30", "c31", "c32", "lP", "lQ"], ["val3"])
+    unit("Ee")
+    unit("Eo")
+    quant("V", 0, 128, T.tv[:], ["tv"], ["qV"])
+    unpack(4, "B0", 0, R, ["qB0a"])
+    window("vvvv", 4, T.wB, WN, 0, R, "wBa")
+
+    mode("1", T.wB, WN, ["wBo%d", "wBa%d"], T.oP1, "oP1", T.gC, "gC", "tA", lambda: None, ("vvss", "ssss"))
+    compose("ssss", T.cA, T.tA, T.oA, "A", whole("tA"))
+
+    spare.extend([lambda: None, lambda: cp("v", T.oP2[:], T.lP[:, SW:], ["lP"], ["oP2"]), lambda: cp("v", T.oK2[:], T.lQ[:, SW:], ["lQ"], ["oK2"]),
+                  lambda: quant("A", R, C, T.tA[:], whole("tA"), ["qAo"])])
+    sort_a(T.lQ[:, SW:], "lQ")
+    sort_b()
+    flush()
+    unpack(0, "A", R, C, ["qAo"])
+    post(T.cA, "A", "aA")
+    window("ssss", 0, T.wA, WN, R, C, "wAo")
+    store(0, "A", R, ["qAo"], "yy")
+    sort_c()
+    unpack(4, "A", 0, R, ["qAa"])
+    window("ssss", 4, T.wA, WN, 0, R, "wAa")
+    for c in range(2):
+        for b in range(4):
+            for n in range(2):
+                f = 2 * C * b + C * n + CH[c][0]
+                cp("s", T.gA[:, f:f + CH[c][1]], listed(T.wA, WN, b, T.oP2, n, c), ["wAo%d" % b, "wAa%d" % b, "oP2"], ["gA%d%d%d" % (b, n, c)])
+    cp("v", T.row3[:].indirect(T.oT[:]), T.val3[:], ["oT", "val3", "c30", "c31", "c32", "row3f0", "row3f1"], ["row3"])
+    dma("y", [(T.dupe[0:128:32, :], T.row3[0:128:32, :]), (T.dupe[16:128:32, :], T.row3[0:128:32, :]),
+              (T.dupo[0:128:32, :], T.row3[16:128:32, :]), (T.dupo[16:128:32, :], T.row3[16:128:32, :])], ["row3"], ["dup"])
+    dma("y", [(T.mJ[:], T.row3[3:128:16, :])], ["row3"], ["mJ"])
+    dma("y", [(T.mK[:], T.row3[8:128:16, :])], ["row3"], ["mK"])
+    dma("y", [(T.fE[:], T.dupe[0:128:16, :]), (T.fO[:], T.dupo[0:128:16, :])], ["dup"], ["fEO"])
+    send_list(T.mK, T.rK3, "aK3", ["mK"], "rK3")
+
+    def hand_on():
+        by_element(T.oB1, T.mJ[:, 0:SW], 0, ["mJ"], "oB1")
+        cp("v", T.oF[:, 0:SW], T.fE[:, 0:SW], ["fEO"], ["oF0"])
+        cp("v", T.oF[:, SW:], T.fO[:, 0:SW], ["fEO"], ["oF1"])
+        cp("v", T.qF[:].bitcast(dt.uint32), T.qA[:].bitcast(dt.uint32).indirect(T.oF[:]), ["qAo", "qAa", "oF0", "oF1"], ["qF"])
+        cp("s", T.sF[:], T.sA[:].indirect(T.oF[:]), ["qAo", "qAa", "oF0", "oF1"], ["sF"])
+        six = [(t, p) for t in order for p in range(2)]
+        e8 = ne // 8
+        cut = [eng[e8 * k:e8 * k + e8] for k in range(4)] + [eng[4 * e8:6 * e8], eng[6 * e8:]]
+        for x, f in (("q", u8), ("s", lambda a: a)):
+            remote([([t], es, f(T[x + "F"][:, R * p + SL * t:R * p + SL * t + SL]), f(T[x + "LF"][:, R * p + SL * (N - 2 - t):R * p + SL * (N - 1 - t)]))
+                    for (t, p), es in zip(six, cut)], "aF", [x + "F"])
+        landed("aF", 2 * got, ["qLF"])
+        mm(4, "V", 0, "A", R, C, ["qV", "qAo"])
+        cp("s", T.yt[:, 0:C], bank(4, C), ["ps4"], ["yt0"])
+
+    mode("2", T.wC, N * C, wCk, T.oK2, "oK2", T.gA, "gA", "tB", hand_on, ("ssss", "ssss"))
+    compose("ssss", T.cB1, T.tB, T.oB1, "B1", whole("tB"))
+    place(T.rK3[:], "rK3")
+    cp("v", T.row3[:].indirect(T.oH[:]), T.pos3[:], ["oH", "pos3"], ["row3"])
+    dma("y", [(T.mP[:], T.row3[3:128:16, :])], ["row3"], ["mP"])
+    quant("B1", R, C, T.tB[:], whole("tB"), ["qB1o"])
+    unpack(0, "B1", R, C, ["qB1o"])
+    post(T.cB1, "B1", "aB1")
+    store(1, "B1", R, ["qB1o"], "yy")
+
+    for b in range(4):
+        for n in range(2):
+            a = W3 * b + C * n
+            f = 2 * C * b + C * n
+            tt(T.w3[:, a:a + C], bank(b, C), T.gA[:, f:f + C], MUL, ["ps%d" % b, "gA%d%d0" % (b, n), "gA%d%d1" % (b, n)], ["w3%d%d" % (n, b)])
+    for b in range(4):
+        mm(4 + b, "Ee", 128 * b, "LF", 0, R, ["qEe%d" % b, "qLF"], True, False)
+        mm(4 + b, "Eo", 128 * b, "LF", R, R, ["qEo%d" % b, "qLF"], False, True)
+    window("ssss", 4, T.fA, R, 0, R, "fA")
+    mm(0, "V", 0, "B1", R, C, ["qV", "qB1o"])
+    cp("s", T.yt[:, C:2 * C], bank(0, C), ["ps0"], ["yt1"])
+    dma("y", [(T.y[:, 0:2 * C], T.yt[:, 0:2 * C])], ["yt0", "yt1"], [])
+    unpack(4, "B1", 0, R, ["qB1a"])
+    for n in range(2):
+        ts(T.oP3[:, h * n:h * n + h], T.mP[:, SW + h * n:SW + h * n + h], float(C * n), None, ADD, None, ["mP"], ["oP3%d" % n])
+    for b in range(4):
+        tt(T.w3[:, W3 * b + 2 * C:W3 * (b + 1)], bank(4 + b, R), T.fA[:, R * b:R * b + R], MUL, ["ps%d" % (4 + b), "fA%d" % b], ["w3a%d" % b])
+    for c in range(2):
+        a, k = CH[c]
+        for b in range(4):
+            cp("s", T.g3[:, C * b + a:C * b + a + k], listed(T.w3, W3, b, T.oP3, 0, c),
+               ["w30%d" % b, "w31%d" % b, "w3a%d" % b, "oP30"], ["g3%d%d" % (c, b)])
+    for c in range(2):
+        a, k = CH[c]
+        for b in range(4):
+            tt(T.m3[:, 4 * a + b:4 * (a + k):4], listed(T.w3, W3, b, T.oP3, 1, c), T.g3[:, C * b + a:C * b + a + k], ADD,
+               ["w30%d" % b, "w31%d" % b, "w3a%d" % b, "oP31", "g3%d%d" % (c, b)], ["M3%d%d" % (c, b)])
+        layer("M3", T.m3[:, 4 * a:4 * (a + k)], "tC", c, 4 * c, ("ssss", "vvss")[c], ["M3%d%d" % (c, b) for b in range(4)])
+    for c in range(2):
+        a, k = CH[c]
+        quant("C1", a, k, T.tC[:, 4 * a:4 * (a + k)], ["tC%d%d" % (c, b) for b in range(4)], ["qC1%d" % c])
+        mm(c, "V", 0, "C1", a, k, ["qV", "qC1%d" % c])
+    store(2, "C1", 0, ["qC10", "qC11"], "yy")
+    for c in range(2):
+        a, k = CH[c]
+        cp("sv"[c], T.yt[:, 2 * C + a:2 * C + a + k], bank(c, k), ["ps%d" % c], ["yt2%d" % c])
+    dma("s", [(T.y[:, 2 * C:], T.yt[:, 2 * C:])], ["yt20", "yt21"], [])
+
+    need("y", list(total.items()))

@@ -30,7 +30,7 @@ _sb(U8, **{"s" + k: n for k, n in _PAIRS.items()})
 _sb(BF, txb=4 * C, pxb=4 * C, txc=4 * C, tv=512, tE=516, tEe=516, tEo=516, one=8 * ROW, wC=4 * N * C, wB=4 * WN, wA=4 * WN, w3=4 * W3,
     gC=8 * C, gA=8 * C, g3=4 * C, p1=4 * C, p2=4 * C, n1=512, n2=512, fA=4 * R, m1=4 * C, m2=4 * C, m3=4 * C,
     tA=4 * C, tB=4 * C, tC=4 * C, cB0=4 * R, cA=4 * R, cB1=4 * R)
-_sb(F32, yt=3 * C, msk=8, mskD=2, r24=160, r16=160, row1=16 * ROW, row3=16 * ROW, val3=2 * C, tab=N * C, pos1=R, pos3=R, val2=R,
+_sb(F32, yt=3 * C, msk=8, mskD=2, r24=160, r16=160, row1=16 * ROW, row3=16 * ROW, val3=2 * C, tab=N * C, pos1=R, pos3=R, val2=2 * R,
     kM=192, kS=160, kY=192, kZ=160, kX=160, kU=192, kV=192, kA=2 * LW, kT=96,
     lJ=ROW, lK=ROW, lI=ROW, rJ=SW, rK=SW, lP=ROW, lQ=ROW, mJ=ROW, mK=ROW, rK3=SW, mP=ROW, dupe=16 * ROW, dupo=16 * ROW,
     fE=ROW, fO=ROW, hE=SW, u1=2 * LW)
@@ -203,8 +203,8 @@ def rank_program(g, core, T, topo):
     def rows(row, part, src, a=0):
         return [(row[part:128:16, 256 * u:256 * u + 256], src[:, a + 16 * u:a + 16 * u + 16]) for u in range(3)]
 
-    def unit(name):
-        for b in range(4):
+    def unit(name, bs=range(4)):
+        for b in bs:
             quant(name, 128 * b, 128, T["t" + name][:, 3 - b:515 - b], ["t" + name], ["q%s%d" % (name, b)])
 
     def by_element(out, src, base, reads, key, bs=range(4)):
@@ -260,11 +260,13 @@ def rank_program(g, core, T, topo):
         tt(L[4], L[3], L[2], ADD, ["hR", "hL1"], ["hT"])
         cp("v", T.oH[:], L[4], ["hT"], ["oH"])
 
-    def layer(m, src, tile, c, b0, es, reads):
+    def layer(m, src, tile, c, b0, es, reads, then=None):
         a, n = CH[c]
         quant(m, a, n, src, reads, ["q%s%d" % (m, c)])
         for b in range(4):
             mm(b0 + b, "W", 128 * b, m, a, n, ["qW", "q%s%d" % (m, c)])
+        if then:
+            then()
         for b in range(4):
             out, reads, writes = T[tile][:, 4 * a + b:4 * (a + n):4], ["ps%d" % (b0 + b)], ["%s%d%d" % (tile, c, b)]
             if es[b] == "v":
@@ -323,7 +325,6 @@ def rank_program(g, core, T, topo):
     fill(T.r16[:, 0:160:16], 0.0, ["r16"])
     for k in range(4):
         fill(T.msk[32 * k:32 * k + 16, 2:3], 1.0, ["msk2"] if k in (0, 3) else [])
-    unit("E")
     for row in ("row1", "row3"):
         for k in range(2):
             act(T[row][:, 8 * ROW * k:8 * ROW * (k + 1)], T.one[:], EMPTY, 0.0, ["one"], [row + "f%d" % k])
@@ -341,32 +342,36 @@ def rank_program(g, core, T, topo):
     cS = ["cS%d" % k for k in range(4)]
     for k in range(4):
         iota(T.cS[32 * k:32 * k + 32, 0:3], [[32, 3]], 0, 1, [cS[k]], reads=["tE", "c10", "c11", "c12"])
+    spare.extend([lambda: unit("E", (0,)), lambda: unit("E", (1, 2)), lambda: unit("E", (3,))])
+    sort_b()
+    flush()
     unpack(0, "C0", lo, C, ["qC0%d" % rank])
     window("ssss", 0, T.wC, N * C, lo, C, "wC%d" % rank)
     for b in range(4):
         cp("s", T.pxb[:, C * b:C * b + C], T.txb[:, b:4 * C:4], ["txb"], ["pxb%d" % b])
-    sort_b()
-    spare.extend([lambda: None, lambda: None, lambda: None,
+    spare.extend([lambda: None, lambda: None,
                   lambda: op("v", lambda: g.vector.tensor_reduce(T.msk[:, 4:5], T.tE[:, 35:516:64], AxisListType.X, ADD), ["tE"], ["msk4"]),
                   lambda: cp("v", T.oK1[:], T.kw[:], ["kw"], ["oK1"]),
                   lambda: cp("v", T.oS[:, 0:3], T.cS[:, 0:3], cS, ["oS"])])
     sort_c()
     cp("v", T.row1[:].indirect(T.oT[:]), T.val1[:], ["oT", "val1", "c10", "c11", "c12", "row1f0", "row1f1"], ["row1"])
     near = [peers[t] for t in order]
-    dma("y", [(u8(T.qW[:]), T.wc[:]), (T.sW[:], T.ws[:])], ["qC0%d" % near[0]], ["qW"])
     dma("y", [(T.lJ[:], T.row1[1:128:16, :])], ["row1"], ["lJ"])
     dma("y", [(T.lK[:], T.row1[8:128:16, :])], ["row1"], ["lK"])
     dma("y", [(T.lI[:], T.row1[0:128:16, :])], ["row1"], ["lI"])
-    dma("y", [(T.tv[:], T.v[:])], ["qC0%d" % near[2]], ["tv"])
-    iota(T.pos1[:], [[1, R]], 0, 0, ["pos10"], True, cS)
-    iota(T.tab[:], [[1, N * C]], 0, 0, ["tab0"], True)
-    iota(T.cD[:, 0:SW], [[16, SW]], 0, 1, ["cD0"])
+    iota(T.cD[:, 0:SW], [[16, SW]], 0, 1, ["cD0"], reads=cS)
     iota(T.cD[:, 2 * SW:3 * SW], [[0, N - 1], [C, 2], [0, S // 16]], R - lo, 0, ["cC"])
+    iota(T.pos1[:], [[1, R]], 0, 0, ["pos10"], True)
+    iota(T.tab[:], [[1, N * C]], 0, 0, ["tab0"], True)
     send_list(T.lJ, T.rJ, "aJ", ["lJ"], "rJ")
     send_list(T.lK, T.rK, "aK", ["lK"], "rK")
     own_columns(T.val3, 0, "c3", True)
     iota(T.pos3[:], [[SL, N - 1], [S - C, 2], [1, S]], 2 * C, 0, ["pos3"], True)
 
+    act(T.msk[:, 5:6], T.msk[:, 4:5], 1.0, -1.0, ["msk4"], ["msk5"])
+    act(T.pos1[:], T.pos1[:], 0.0, T.msk[:, 5:6], ["pos10", "msk5"], ["pos1"])
+    unpack(4, "C0", C * near[0], C, ["qC0%d" % near[0]])
+    window("ssss", 4, T.wC, N * C, C * near[0], C, "wC%d" % near[0])
     quant("B0", R, C, T.txb[:], ["txb"], ["qB0o"])
     ts(T.cD[:, 3 * SW:3 * SW + 1], T.cD[:, 0:1], 112, None, AND, None, ["cD0"], ["cp1"])
     ts(T.u1[:, 0:LW], T.kG[:], float(WN), float(C), AluOpType.is_ge, MUL, ["kG"], ["u1"])
@@ -374,40 +379,43 @@ def rank_program(g, core, T, topo):
     tt(T.u1[:, LW:], T.kG[:], T.u1[:, 0:LW], SUB, ["kG", "u1"], ["u2"])
     ts(T.cD[:, SW:2 * SW], T.cD[:, 0:SW], T.mskD[:, 0:1], None, SUB, None, ["cD0", "msk0"], ["cD"])
     cp("v", T.oP1[:], T.u1[:, LW:], ["u2"], ["oP1"])
-    unpack(4, "C0", C * near[0], C, ["qC0%d" % near[0]])
-    window("ssss", 4, T.wC, N * C, C * near[0], C, "wC%d" % near[0])
     unpack(0, "C0", C * near[1], C, ["qC0%d" % near[1]])
-    window("ssvv", 0, T.wC, N * C, C * near[1], C, "wC%d" % near[1])
+    window("vvvv", 0, T.wC, N * C, C * near[1], C, "wC%d" % near[1])
     unpack(4, "C0", C * near[2], C, ["qC0%d" % near[2]])
-    window("ssvv", 4, T.wC, N * C, C * near[2], C, "wC%d" % near[2])
+    window("ssvs", 4, T.wC, N * C, C * near[2], C, "wC%d" % near[2])
     unpack(0, "B0", R, C, ["qB0o"])
-    window("vvvs", 0, T.wB, WN, R, C, "wBo")
-    act(T.msk[:, 5:6], T.msk[:, 4:5], 1.0, -1.0, ["msk4"], ["msk5"])
-    act(T.tab[:], T.tab[:], 0.0, T.msk[:, 4:5], ["tab0", "msk4"], ["tab"])
-    act(T.pos1[:], T.pos1[:], 0.0, T.msk[:, 5:6], ["pos10", "msk5"], ["pos1"])
+    window("vvvv", 0, T.wB, WN, R, C, "wBo")
+    wCk = ["wC%d" % o + "%d" for o in range(N)]
+
+    def gather_c(b):
+        cp("s", T.gC[:, 2 * C * b:2 * C * (b + 1)], T.wC[:, N * C * b:N * C * (b + 1)].indirect(T.oK1[:]),
+           [k % b for k in wCk] + ["oK1"], ["gC%d%d%d" % (b, n, c) for n in range(2) for c in range(2)])
+
+    gather_c(0)
 
     ts(T.oB0[:], T.rJ[:], float(lo), None, SUB, None, ["rJ"], ["oB0"])
     for b in (0, 2, 1, 3):
         cp("vvss"[b], T.cB0[:, b:4 * R:4], T.pxb[:, C * b:C * b + C].indirect(T.oB0[:]), ["pxb%d" % b, "oB0"], ["cB0%d" % b])
     post(T.cB0, "B0", "aB0")
-    wCk = ["wC%d" % o + "%d" for o in range(N)]
-    for b in range(4):
-        cp("s", T.gC[:, 2 * C * b:2 * C * (b + 1)], T.wC[:, N * C * b:N * C * (b + 1)].indirect(T.oK1[:]),
-           [k % b for k in wCk] + ["oK1"], ["gC%d%d%d" % (b, n, c) for n in range(2) for c in range(2)])
-    spare.extend([lambda t=t: by_element(T.oA, T.lI[:, 0:SW], R, ["lI"], "oA", (t,)) for t in range(4)]
-                 + [lambda: cp("v", T.oK[:], T.rK[:], ["rK"], ["oK"])])
+    gather_c(1)
+    cp("v", T.oK[:], T.rK[:], ["rK"], ["oK"])
+    act(T.val2[:, R:], T.tab[:].indirect(T.oK[:]), 0.0, T.msk[:, 4:5], ["tab0", "oK", "msk4"], ["hV"])
+    gather_c(2)
+    gather_c(3)
+    spare.extend([lambda t=t: by_element(T.oA, T.lI[:, 0:SW], R, ["lI"], "oA", (t,)) for t in range(4)])
     place(T.rJ[:], "rJ")
     flush()
-    tt(T.val2[:], T.tab[:].indirect(T.oK[:]), T.pos1[:], ADD, ["tab", "oK", "pos1"], ["val2"])
-    cp("v", T.row1[:].indirect(T.oH[:]), T.val2[:], ["oH", "val2"], ["row1"])
-    dma("y", [(T.lQ[:], T.row1[8:128:16, :])], ["row1"], ["lQ"])
-    dma("y", [(T.lP[:], T.row1[0:128:16, :])], ["row1"], ["lP"])
-    dma("y", rows(T.val3, 0, T.lP, SW) + rows(T.val3, 8, T.lQ, SW), ["c30", "c31", "c32", "lP", "lQ"], ["val3"])
+    tt(T.val2[:, 0:R], T.val2[:, R:], T.pos1[:], ADD, ["hV", "pos1"], ["val2"])
+    cp("v", T.row1[:].indirect(T.oH[:]), T.val2[:, 0:R], ["oH", "val2"], ["row1"])
     unit("Ee")
     unit("Eo")
-    quant("V", 0, 128, T.tv[:], ["tv"], ["qV"])
     unpack(4, "B0", 0, R, ["qB0a"])
-    window("vvvv", 4, T.wB, WN, 0, R, "wBa")
+    window("vsvs", 4, T.wB, WN, 0, R, "wBa")
+    dma("y", [(T.lQ[:], T.row1[8:128:16, :])], ["row1"], ["lQ"])
+    dma("y", [(T.lP[:], T.row1[0:128:16, :])], ["row1"], ["lP"])
+    dma("y", [(u8(T.qW[:]), T.wc[:]), (T.sW[:], T.ws[:])], ["qB0a"], ["qW"])
+    dma("y", rows(T.val3, 0, T.lP, SW) + rows(T.val3, 8, T.lQ, SW), ["c30", "c31", "c32", "lP", "lQ"], ["val3"])
+    dma("y", [(T.tv[:], T.v[:])], [], ["tv"])
 
     mode("1", T.wB, WN, ["wBo%d", "wBa%d"], T.oP1, "oP1", T.gC, "gC", "tA", lambda: None, ("vvss", "ssss"))
     compose("ssss", T.cA, T.tA, T.oA, "A", whole("tA"))
@@ -420,7 +428,6 @@ def rank_program(g, core, T, topo):
     unpack(0, "A", R, C, ["qAo"])
     post(T.cA, "A", "aA")
     window("ssss", 0, T.wA, WN, R, C, "wAo")
-    store(0, "A", R, ["qAo"], "yy")
     sort_c()
     unpack(4, "A", 0, R, ["qAa"])
     window("ssss", 4, T.wA, WN, 0, R, "wAa")
@@ -436,11 +443,13 @@ def rank_program(g, core, T, topo):
     dma("y", [(T.mK[:], T.row3[8:128:16, :])], ["row3"], ["mK"])
     dma("y", [(T.fE[:], T.dupe[0:128:16, :]), (T.fO[:], T.dupo[0:128:16, :])], ["dup"], ["fEO"])
     send_list(T.mK, T.rK3, "aK3", ["mK"], "rK3")
+    store(0, "A", R, ["qAo", "qAa"], "yy")
 
     def hand_on():
         by_element(T.oB1, T.mJ[:, 0:SW], 0, ["mJ"], "oB1")
         cp("v", T.oF[:, 0:SW], T.fE[:, 0:SW], ["fEO"], ["oF0"])
         cp("v", T.oF[:, SW:], T.fO[:, 0:SW], ["fEO"], ["oF1"])
+        quant("V", 0, 128, T.tv[:], ["tv"], ["qV"])
         cp("v", T.qF[:].bitcast(dt.uint32), T.qA[:].bitcast(dt.uint32).indirect(T.oF[:]), ["qAo", "qAa", "oF0", "oF1"], ["qF"])
         cp("s", T.sF[:], T.sA[:].indirect(T.oF[:]), ["qAo", "qAa", "oF0", "oF1"], ["sF"])
         six = [(t, p) for t in order for p in range(2)]
@@ -461,7 +470,13 @@ def rank_program(g, core, T, topo):
     quant("B1", R, C, T.tB[:], whole("tB"), ["qB1o"])
     unpack(0, "B1", R, C, ["qB1o"])
     post(T.cB1, "B1", "aB1")
-    store(1, "B1", R, ["qB1o"], "yy")
+
+    def last(c):
+        a, k = CH[c]
+        quant("C1", a, k, T.tC[:, 4 * a:4 * (a + k)], ["tC%d%d" % (c, b) for b in range(4)], ["qC1%d" % c])
+        mm(c, "V", 0, "C1", a, k, ["qV", "qC1%d" % c])
+        cp("s", T.yt[:, 2 * C + a:2 * C + a + k], bank(c, k), ["ps%d" % c], ["yt2%d" % c])
+        dma("s", [(T.y[:, 2 * C + a:2 * C + a + k], T.yt[:, 2 * C + a:2 * C + a + k])], ["yt2%d" % c], [])
 
     for b in range(4):
         for n in range(2):
@@ -474,8 +489,9 @@ def rank_program(g, core, T, topo):
     window("ssss", 4, T.fA, R, 0, R, "fA")
     mm(0, "V", 0, "B1", R, C, ["qV", "qB1o"])
     cp("s", T.yt[:, C:2 * C], bank(0, C), ["ps0"], ["yt1"])
-    dma("y", [(T.y[:, 0:2 * C], T.yt[:, 0:2 * C])], ["yt0", "yt1"], [])
     unpack(4, "B1", 0, R, ["qB1a"])
+    dma("y", [(T.y[:, 0:2 * C], T.yt[:, 0:2 * C])], ["yt0", "yt1", "qB1a"], [])
+    store(1, "B1", R, ["qB1o", "qB1a"], "yy")
     for n in range(2):
         ts(T.oP3[:, h * n:h * n + h], T.mP[:, SW + h * n:SW + h * n + h], float(C * n), None, ADD, None, ["mP"], ["oP3%d" % n])
     for b in range(4):
@@ -490,15 +506,9 @@ def rank_program(g, core, T, topo):
         for b in range(4):
             tt(T.m3[:, 4 * a + b:4 * (a + k):4], listed(T.w3, W3, b, T.oP3, 1, c), T.g3[:, C * b + a:C * b + a + k], ADD,
                ["w30%d" % b, "w31%d" % b, "w3a%d" % b, "oP31", "g3%d%d" % (c, b)], ["M3%d%d" % (c, b)])
-        layer("M3", T.m3[:, 4 * a:4 * (a + k)], "tC", c, 4 * c, ("ssss", "vvss")[c], ["M3%d%d" % (c, b) for b in range(4)])
-    for c in range(2):
-        a, k = CH[c]
-        quant("C1", a, k, T.tC[:, 4 * a:4 * (a + k)], ["tC%d%d" % (c, b) for b in range(4)], ["qC1%d" % c])
-        mm(c, "V", 0, "C1", a, k, ["qV", "qC1%d" % c])
+        layer("M3", T.m3[:, 4 * a:4 * (a + k)], "tC", c, 4 * c, ("ssss", "vvvv")[c], ["M3%d%d" % (c, b) for b in range(4)],
+              (None, lambda: last(0))[c])
+    last(1)
     store(2, "C1", 0, ["qC10", "qC11"], "yy")
-    for c in range(2):
-        a, k = CH[c]
-        cp("sv"[c], T.yt[:, 2 * C + a:2 * C + a + k], bank(c, k), ["ps%d" % c], ["yt2%d" % c])
-    dma("s", [(T.y[:, 2 * C:], T.yt[:, 2 * C:])], ["yt20", "yt21"], [])
 
     need("y", list(total.items()))

@@ -1,48 +1,68 @@
 from concourse.bass import DstId, RemoteDMATransfer
-from concourse.mybir import dt, AluOpType, AxisListType, ActivationFunctionType
+from concourse.mybir import dt, AluOpType, ActivationFunctionType
 
 N = 4
 C = 384
 S = 48
 SL = 2 * S
 R = (N - 1) * SL
-CH = ((0, 256), (256, 128))
+CH = ((0, 192), (192, 192))
+CH3 = ((0, 256), (256, 128))
 LW = 2 * C // 16
+h = LW // 2
 SW = R // 16
 ROW = SW + LW
 WN = R + C
 W3 = 2 * C + R
-EMPTY = -4096.0
+G = h + 1
+OWN1 = 2048
+OWN3 = 1808
+T2 = R + 32
 
 X4, U8, BF, F32, I32, U16 = "float8_e4m3fn_x4", "uint8", "bfloat16", "float32", "int32", "uint16"
-SCRATCH = {"ps": ("psum", [128, 4096], F32), "kD": ("sbuf", [128, 3, 32], F32)}
+SCRATCH = {"ps": ("psum", [128, 4096], F32), "dK": ("dram", [N - 1, 128, SL // 16], F32), "dL": ("dram", [N - 1, 128, SL // 16], F32)}
 
 
 def _sb(dtype, **kw):
     for name, n in kw.items():
-        SCRATCH[name] = ("sbuf", [128, n], dtype)
+        SCRATCH[name] = ("sbuf", [128] + (list(n) if isinstance(n, tuple) else [n]), dtype)
 
 
 _PAIRS = dict(W=512, V=128, E=512, Ee=512, Eo=512, C0=N * C, B0=WN, A=WN, B1=WN, C1=C, M1=C, M2=C, M3=C,
               sB0=R, sA=R, sB1=R, F=2 * R, LF=2 * R)
 _sb(X4, **{"q" + k: n for k, n in _PAIRS.items()})
 _sb(U8, **{"s" + k: n for k, n in _PAIRS.items()})
-_sb(BF, txb=4 * C, pxb=4 * C, txc=4 * C, tv=512, tE=516, tEe=516, tEo=516, one=8 * ROW, wC=4 * N * C, wB=4 * WN, wA=4 * WN, w3=4 * W3,
-    gC=8 * C, gA=8 * C, g3=4 * C, p1=4 * C, p2=4 * C, n1=512, n2=512, fA=4 * R, m1=4 * C, m2=4 * C, m3=4 * C,
+_sb(BF, txb=4 * C, txc=4 * C, tv=512, tE=516, tEe=516, tEo=516, one=128, c80=T2, wC=4 * N * C, wB=4 * WN, wA=4 * WN, w3=4 * W3,
+    gC=(8, C), gA=(8, C), g3=4 * C, m1=8 * C, m2=8 * C, fA=4 * R, m3=4 * C,
     tA=4 * C, tB=4 * C, tC=4 * C, cB0=4 * R, cA=4 * R, cB1=4 * R)
-_sb(F32, yt=3 * C, msk=8, mskD=2, r24=160, r16=160, row1=16 * ROW, row3=16 * ROW, val3=2 * C, tab=N * C, pos1=R, pos3=R, val2=2 * R,
-    kM=192, kS=160, kY=192, kZ=160, kX=160, kU=192, kV=192, kA=2 * LW, kT=96,
-    lJ=ROW, lK=ROW, lI=ROW, rJ=SW, rK=SW, lP=ROW, lQ=ROW, mJ=ROW, mK=ROW, rK3=SW, mP=ROW, dupe=16 * ROW, dupo=16 * ROW,
-    fE=ROW, fO=ROW, hE=SW, u1=2 * LW)
-_sb(I32, jw=LW, kw=LW, val1=2 * C, cD=4 * SW, cS=4, kO=LW, kG=LW, kL=2 * LW, kR=LW, hL=5 * SW)
-_sb(U16, oS=4, oT=LW, oH=SW, oK=SW, oK1=LW, oP1=LW, oP2=LW, oK2=LW, oP3=LW, oB0=SW, oA=4 * SW, oB1=4 * SW, oF=2 * SW)
+_sb(F32, yt=3 * C, row1=OWN1 + 2 * C, row3=OWN3 + 16 * ROW, val2=R, val3=2 * C, pos3=R, rr=6 * G + 32, cz=736, zrow=160, srow=(2, LW), cc=8,
+    cK=6, ch=SW, kM=8 * G, kS=6 * G, kU=8 * G, kV=(8, G), kA=(4, G), kW=(2, G), kD=(3, 32), kZ=64, kT=96, kF=48, kI=(3, 16), ka=LW, kb=LW,
+    rJ=SW, lP=LW, lQ=LW, l3=(6, h), mJ=ROW, mK=ROW, rK3=SW, mP=ROW, dupe=16 * ROW, dupo=16 * ROW, fE=ROW, fO=ROW, u1=LW, ha=SW, hb=SW)
+_sb(I32, jw=LW, kw=(2, h), val1=2 * C, kO=(2, G), kG=LW, kq=LW, hq=SW)
+_sb(U16, oS=4, oX=4, oT=LW, oH=SW, oK1=LW, oP1=LW, oP2=LW, oK2=LW, oP3=LW, oB0=4 * SW, oA=4 * SW, oB1=4 * SW, oF=2 * SW)
 
 SEMAPHORES = (["cv", "cs", "ct", "cg", "sent", "aJ", "aK", "aK3", "aB0", "aA", "aB1", "aF"]
-              + ["aC%d" % k for k in range(N)] + ["d%d" % k for k in range(48)])
+              + ["aC%d" % k for k in range(N)] + ["d%d" % k for k in range(64)])
 
 ADD, SUB, MUL, MAX, MIN = AluOpType.add, AluOpType.subtract, AluOpType.mult, AluOpType.max, AluOpType.min
-EQ, AND, SHR = AluOpType.is_equal, AluOpType.bitwise_and, AluOpType.arith_shift_right
+EQ, SHR = AluOpType.is_equal, AluOpType.arith_shift_right
 COPY, IDENT = ActivationFunctionType.Copy, ActivationFunctionType.Identity
+
+PLAN = (
+    "0 11 3 1 4 5 19y 16s 12 6 15s 7 25 21 8 31 10 17s 32 9 26 30 24 14 56 23 18y 68 13 59 22 2y 57 58 69 70 61 42 62s 27 60 29 63 50 33 64 101 43 54s 20y "
+    "65 71 102 179y 66 28 103 72 49 44 67 155 104 73 48 74 51 106s 105 80 107s 82 81 75 53s 83 76 84 45 77 52s 85 46 108s 110 47 119 112 109s 111 118 55s "
+    "114s 113 120 115s 126 116s 122s 128 121 86y 88 124s 87 117s 89v 40 92 98v 90 97 129 123v 127 93 100 99 91 181 94 161 145 143 142 149s 144 147v 95 "
+    "96y 148s 146v 163v 132s 150 162 130s 79 151 78 152 37 154 38 133s 164 160 165 39 166 136s 41 153 167 171 134v 125s 168 156 138s 174 173 172 137s "
+    "131s 175v 169y 170y 182 178s 177s 196 176s 180y 185 135s 184 139s 183 141s 197 186 140s 199 240s 198 239s 227 158 200 228 229 230 232 157 35 233s 34 "
+    "242s 234 241s 235 187 236 191 189 237 188 231 190 244 192s 238 36 195s 247 193s 201 194s 248 205 204 246 202 209s 203 208v 206s 207v 249 210s 218 "
+    "250 213s 159 294y 220 252 221 251 296y 212v 219 211s 222 253 254 223s 214 255 245 215 305 216 256 243 306s 257 293s 295s 217 225s 280 277 279 278 "
+    "226s 224s 284s 283s 282s 286s 281v 258y 260y 285v 287s 259y 288s 307 262 308 289s 263 309 261y 290s 297y 310 291s 321 311 292s 322 265s 323 324 298 "
+    "299 325 264 267 301s 312 266 274 313 275 314 268 316 315 300 318s 303 319s 269 320s 276 302 273 326 317s 270 328 327 330 332s 329 331s 334s 304 333v "
+    "271y 343 338s 335v 336s 344 378y 345 379y 347 348 337s 356 360 361 358 349 357 376s 362 363 375s 359 339 346 366s 368 350 340 377s 341 364s 351 367s "
+    "354 342 365s 355 369s 272 371 352 370 372 373 374s 353 381 380 386s 382 384s 383 387 388s 385 390s 389 401s 391 407s 402 405s 392 403s 406 394 408 "
+    "393 396 398s 395 404 397s 409 400v 413 399s 410 412 411 417v 414s 418 416s 415v 426y 419 422s 427 424y 423s 420v 431y 432s 428 429v 425s 421y 435s "
+    "430y 434s 433y"
+)
 
 
 def rank_program(g, core, T, topo):
@@ -53,72 +73,74 @@ def rank_program(g, core, T, topo):
     peers = [(rank + 1 + t) % N for t in range(N - 1)]
     pcore = [T.cores[o] for o in peers]
     Q = {"v": g.vector, "s": g.scalar, "t": g.tensor, "g": g, "y": g.sync}
-    total, waited, writer, readers, free, spare = {}, {}, {}, {}, [0, 0], []
+    steps, writer, readers, count = [], {}, {}, {"sent": 0, "dma": 0}
 
-    def need(e, toks):
-        top = {}
-        for s, v in toks:
-            top[s] = max(top.get(s, 0), v)
-        for s, v in top.items():
-            if waited.get((e, s), 0) < v:
-                Q[e].wait_ge(T.sem[s], v)
-                waited[(e, s)] = v
-
-    def deps(e, reads, writes, more=False):
-        toks = []
+    def note(es, call, reads, writes, more=False, sem=None):
+        me, before = len(steps), {}
         for k in reads:
-            toks.append(writer[k])
+            before[writer[k]] = True
+        for k in writes:
+            if k in writer:
+                before[writer[k]] = before.get(writer[k], False) or not more
+            for x in readers.get(k, []):
+                before[x] = True
+        for k in reads:
             if k.startswith("ps"):
-                toks += [t for t in readers.get(k, []) if t[0] != "c" + e]
+                for x in readers.get(k, []):
+                    before.setdefault(x, False)
+            readers.setdefault(k, []).append(me)
         for k in writes:
-            if k in writer and not more:
-                toks.append(writer[k])
-            toks += readers.get(k, [])
-        need(e, toks)
+            writer[k], readers[k] = me, []
+        steps.append(dict(es=es, call=call, before=before, sem=sem))
 
-    def mark(tok, reads, writes):
-        for k in reads:
-            readers.setdefault(k, []).append(tok)
-        for k in writes:
-            writer[k], readers[k] = tok, []
+    def dma(es, moves, reads, writes, add=False):
+        s = "d%d" % count["dma"]
+        count["dma"] += 1
 
-    def op(e, call, reads, writes, more=False):
-        if e == "v" and spare and not free[1] and any(writer[k] == ("cv", total["cv"]) for k in reads):
-            free[1] = 1
-            spare.pop(0)()
-            free[1] = 0
-        deps(e, reads, writes, more)
-        s = "c" + e
-        total[s] = total.get(s, 0) + 1
-        call().then_inc(T.sem[s], 1)
-        mark((s, total[s]), reads, writes)
-
-    def flush():
-        while spare:
-            spare.pop(0)()
-
-    def dma(e, moves, reads, writes, add=False):
-        deps(e, reads, writes)
-        s = "d%d" % free[0]
-        free[0] += 1
-        for out, src in moves:
-            (g.dma_start(out, src, accum_op=ADD) if add else Q[e].dma_start(out, src)).then_inc(T.sem[s], 16)
-        total[s] = 16 * len(moves)
-        mark((s, total[s]), reads, writes)
+        def call(e):
+            for out, src in moves:
+                (g.dma_start(out, src, accum_op=ADD) if add else Q[e].dma_start(out, src)).then_inc(T.sem[s], 16)
+        note(es, call, reads, writes, sem=(s, 16 * len(moves)))
 
     def remote(moves, sem, reads):
-        deps("g", reads, [])
         ts_ = []
         for ts, es, src, dst in moves:
             ids = [DstId(rid=topo.addr(pcore[t])[0], pnc=topo.addr(pcore[t])[1]) for t in ts]
             ts_.append(RemoteDMATransfer(dst_ids=ids, dma_engine_mask=sum(1 << x for x in es), remote_sem=T.sem[sem],
                                          srcs=[src], dsts=[dst] * len(ts)))
-            total["sent"] = total.get("sent", 0) + len(es)
-        g.remote_dma_fused(ts_, local_sem=T.sem.sent)
+            count["sent"] += len(es)
+        note("g", lambda e: g.remote_dma_fused(ts_, local_sem=T.sem.sent), reads, [], sem=("sent", 0))
 
     def landed(sem, n, keys):
-        total[sem] = n
-        mark((sem, n), [], keys)
+        note("", None, [], keys, sem=(sem, n))
+
+    def issue():
+        total, waited = {"sent": count["sent"]}, {}
+        for w in PLAN.split() or [str(k) for k in range(len(steps))]:
+            s = steps[int(w.rstrip("vsyg"))]
+            e = s["e"] = s["es"][:1] if w[-1].isdigit() else w[-1]
+            if s["sem"] is None:
+                total["c" + e] = total.get("c" + e, 0) + 1
+                s["tok"] = ("c" + e, total["c" + e])
+            elif s["sem"][1]:
+                s["tok"] = s["sem"]
+                total[s["sem"][0]] = s["sem"][1]
+            if not e:
+                continue
+            top = {}
+            for x, hard in s["before"].items():
+                if hard or steps[x]["e"] != e:
+                    name, v = steps[x]["tok"]
+                    top[name] = max(top.get(name, 0), v)
+            for name, v in top.items():
+                if waited.get((e, name), 0) < v:
+                    Q[e].wait_ge(T.sem[name], v)
+                    waited[(e, name)] = v
+            done = s["call"](e)
+            if s["sem"] is None:
+                done.then_inc(T.sem[s["tok"][0]], 1)
+        for name, v in total.items():
+            g.sync.wait_ge(T.sem[name], v)
 
     eng = [x for x in topo.engines(core, pcore[0]) if all(x in topo.engines(core, c) for c in pcore)]
     ne = len(eng)
@@ -139,9 +161,11 @@ def rank_program(g, core, T, topo):
         return ap.bitcast(dt.uint8)
 
     def send_list(src, dst, sem, reads, key):
-        w = SL // 16
-        remote([([t], wide[t], src[:, w * t:w * t + w], dst[:, w * (N - 2 - t):w * (N - 1 - t)]) for t in range(N - 1)], sem, reads)
+        remote([([t], wide[t], src(t), dst(N - 2 - t)) for t in range(N - 1)], sem, reads)
         landed(sem, got, [key])
+
+    def block(buf, step=SL // 16):
+        return lambda t: buf[:, step * t:step * t + SL // 16]
 
     def send_slots(src, dst, sem, reads, key):
         at = [(t, SL * t, SL * (N - 2 - t)) for t in range(N - 1)]
@@ -151,32 +175,41 @@ def rank_program(g, core, T, topo):
 
     def ts(out, src, s1, s2, o0, o1, reads, writes):
         if o1 is None:
-            op("v", lambda: g.vector.tensor_scalar(out, src, s1, None, o0), reads, writes)
+            note("v", lambda e: g.vector.tensor_scalar(out, src, s1, None, o0), reads, writes)
         else:
-            op("v", lambda: g.vector.tensor_scalar(out, src, s1, s2, o0, o1), reads, writes)
+            note("v", lambda e: g.vector.tensor_scalar(out, src, s1, s2, o0, o1), reads, writes)
 
     def tt(out, a, b, o, reads, writes):
-        op("v", lambda: g.vector.tensor_tensor(out, a, b, o), reads, writes)
+        note("v", lambda e: g.vector.tensor_tensor(out, a, b, o), reads, writes)
 
-    def cp(e, out, src, reads, writes):
-        if e == "v":
-            op("v", lambda: g.vector.tensor_copy(out, src), reads, writes)
-        else:
-            op("s", lambda: g.scalar.activation(out, src, COPY), reads, writes)
+    def cp(es, out, src, reads, writes):
+        note(es, lambda e: g.vector.tensor_copy(out, src) if e == "v" else g.scalar.activation(out, src, COPY), reads, writes)
 
-    def act(out, src, bias, scl, reads, writes):
-        op("s", lambda: g.scalar.activation(out, src, IDENT, bias=bias, scale=scl), reads, writes)
+    def line(es, out, src, by, plus, reads, writes):
+        def call(e):
+            if e == "s":
+                return g.scalar.activation(out, src, IDENT, bias=plus, scale=by)
+            if plus == 0.0:
+                return g.vector.tensor_scalar(out, src, by, None, MUL)
+            return g.vector.tensor_scalar(out, src, by, plus, MUL, ADD)
+        note(es, call, reads, writes)
 
     def fill(ap, v, writes):
-        op("v", lambda: g.vector.memset(ap, v), [], writes)
+        note("v", lambda e: g.vector.memset(ap, v), [], writes)
+
+    def scan(out, a, b, first, o0, o1, reads, writes):
+        note("v", lambda e: g.vector.tensor_tensor_scan(out, a, b, first, o0, o1), reads, writes)
+
+    def turn(out, src, reads, writes):
+        note("v", lambda e: g.vector.transpose(out, src), reads, writes)
 
     def quant(name, a, n, tile, reads, writes):
-        op("v", lambda: g.vector.quantize_mx(T["q" + name][:, a:a + n], T["s" + name][:, a:a + n], tile), reads, writes)
+        note("v", lambda e: g.vector.quantize_mx(T["q" + name][:, a:a + n], T["s" + name][:, a:a + n], tile), reads, writes)
 
     def mm(bank, w, wa, x, a, n, reads, start=True, stop=True):
-        op("t", lambda: g.tensor.matmul_mx(T.ps[:, 512 * bank:512 * bank + n], T["q" + w][:, wa:wa + 128], T["s" + w][:, wa:wa + 128],
-                                           T["q" + x][:, a:a + n], T["s" + x][:, a:a + n], start, stop),
-           reads, ["ps%d" % bank], more=not start)
+        note("t", lambda e: g.tensor.matmul_mx(T.ps[:, 512 * bank:512 * bank + n], T["q" + w][:, wa:wa + 128], T["s" + w][:, wa:wa + 128],
+                                               T["q" + x][:, a:a + n], T["s" + x][:, a:a + n], start, stop),
+             reads, ["ps%d" % bank], more=not start)
 
     def bank(k, n):
         return T.ps[:, 512 * k:512 * k + n]
@@ -185,330 +218,293 @@ def rank_program(g, core, T, topo):
         for b in range(4):
             mm(b0 + b, "E", 128 * b, x, a, n, ["qE%d" % b] + reads)
 
-    def window(es, b0, win, width, a, n, key):
+    def window(b0, win, width, a, n, key):
         for b in range(4):
-            cp(es[b], win[:, width * b + a:width * b + a + n], bank(b0 + b, n), ["ps%d" % (b0 + b)], ["%s%d" % (key, b)])
+            cp("sv", win[:, width * b + a:width * b + a + n], bank(b0 + b, n), ["ps%d" % (b0 + b)], ["%s%d" % (key, b)])
 
-    def iota(ap, pattern, base, mult, writes, small=False, reads=()):
+    def iota(ap, pattern, base, writes, small=True):
         if small:
-            op("g", lambda: g.iota(ap, pattern, base, mult, allow_small_or_imprecise_dtypes=True), list(reads), writes)
+            note("g", lambda e: g.iota(ap, pattern, base, 0, allow_small_or_imprecise_dtypes=True), [], writes)
         else:
-            op("g", lambda: g.iota(ap, pattern, base, mult), list(reads), writes)
+            note("g", lambda e: g.iota(ap, pattern, base, 0), [], writes)
 
-    def own_columns(row, base, key, small):
-        iota(row[:, 0:256], [[1, 16], [16, 16]], base, 0, [key + "0"], small)
-        iota(row[:, 256:512], [[1, 16], [128 - C, 2], [16, 8]], base + 256, 0, [key + "1"], small)
-        iota(row[:, 512:768], [[1, 16], [16, 16]], base + 512 - C, 0, [key + "2"], small)
-
-    def rows(row, part, src, a=0):
-        return [(row[part:128:16, 256 * u:256 * u + 256], src[:, a + 16 * u:a + 16 * u + 16]) for u in range(3)]
-
-    def unit(name, bs=range(4)):
-        for b in bs:
+    def unit(name):
+        for b in range(4):
             quant(name, 128 * b, 128, T["t" + name][:, 3 - b:515 - b], ["t" + name], ["q%s%d" % (name, b)])
 
-    def by_element(out, src, base, reads, key, bs=range(4)):
-        for t in bs:
+    def by_element(out, src, base, reads, key):
+        for t in range(4):
             ts(out[:, SW * t:SW * t + SW], src, 4.0, float(t - 4 * base), MUL, ADD, reads, ["%s%d" % (key, t)])
 
-    def compose(es, tile, src, off, name, reads):
-        for t in (0, 2, 1, 3):
-            cp(es[t], tile[:, t:4 * R:4], src[:, 0:4 * C].indirect(off[:, SW * t:SW * t + SW]), reads + ["o%s%d" % (name, t)], ["c%s%d" % (name, t)])
+    def compose(tile, src, off, name, reads):
+        for t in range(4):
+            cp("sv", tile[:, t:4 * R:4], src[:, 0:4 * C].indirect(off[:, SW * t:SW * t + SW]), reads + ["o%s%d" % (name, t)], ["c%s%d" % (name, t)])
 
     def post(tile, name, sem):
         quant("s" + name, 0, R, tile[:], ["c%s%d" % (name, t) for t in range(4)], ["qs" + name])
         send_slots("s" + name, name, sem, ["qs" + name], "q%sa" % name)
 
-    km = ["kM%d" % t for t in range(N)]
-    h = LW // 2
+    def chunked(out, src, add, reads, key):
+        for c, (a, k) in enumerate(CH):
+            ts(out[:, a // 8:(a + k) // 8], src[:, :, a // 16:(a + k) // 16], add, None, ADD, None, reads, ["%s%d" % (key, c)])
 
-    def sort_a(X, xk):
-        ts(T.kO[:], X, 1.0 / C, 0.5 / C - 0.5, MUL, ADD, [xk], ["kO"])
-        for n in range(2):
-            ts(T.kU[:, 3 * LW + h * n:3 * LW + h * n + h], X[:, h * n:h * n + h], float(R - lo + C * n), None, ADD, None, [xk], ["kU%d" % (6 + n)])
+    km = ["kM%d" % t for t in range(N - 1)]
+
+    def number(X, xk):
+        ts(T.kO[:, :, 1:G], X, 1.0 / C, 0.5 / C - 0.5, MUL, ADD, [xk, "kOg"], ["kO"])
         for t, o in enumerate(peers + [rank]):
-            ts(T.kM[:, LW * t:LW * t + LW], T.kO[:], float(o), None, EQ, None, ["kO"], ["kM%d" % t])
-        op("v", lambda: g.vector.tensor_tensor_scan(T.kS[:], T.r24[:], T.kM[:, 0:160], 0.0, MUL, ADD), km + ["r24"], ["kS"])
+            ts(T.kM[:, 2 * G * t:2 * G * (t + 1)], T.kO[:], float(o), None, EQ, None, ["kO"], ["kM%d" % t])
+        scan(T.kS[:], T.rr[:, 0:6 * G], T.kM[:, 0:6 * G], 0.0, MUL, ADD, km + ["r25"], ["kS"])
+        cp("vs", T.cz[:, 704:710], T.kS[:, h:6 * G:G], ["kS", "cz"], ["kP"])
+        turn(T.cz[:, 672:704], T.cz[:, 704:736], ["kP"], ["kY"])
+        scan(T.kZ[:, 0:32], T.cz[:, 671:703], T.rr[:, 6 * G:], 0.0, ADD, MUL, ["kY", "r16"], ["kZ"])
+        turn(T.kZ[:, 32:64], T.kZ[:, 0:32], ["kZ"], ["kX"])
+        tt(T.kM[:, 0:6 * G:G], T.kZ[:, 32:38], T.cK[:], ADD, ["kX", "cK"], km)
+        scan(T.kU[:, 0:6 * G], T.rr[:, 0:6 * G], T.kM[:, 0:6 * G], 0.0, MUL, ADD, km, ["kU"])
 
-    def sort_b():
-        op("v", lambda: g.vector.transpose(T.kY[:, 32:192], T.kS[:]), ["kS"], ["kY"])
-        op("v", lambda: g.vector.tensor_tensor_scan(T.kZ[:], T.kY[:, 31:191], T.r16[:], 0.0, ADD, MUL), ["kY", "kYpad", "r16"], ["kZ"])
-        op("v", lambda: g.vector.transpose(T.kX[:], T.kZ[:]), ["kZ"], ["kX"])
-
-    def sort_c():
-        for k in range(2 * (N - 1)):
-            ts(T.kU[:, h * k:h * k + h], T.kS[:, h * k:h * k + h], T.kX[:, h * k + h - 1:h * k + h], float(S * k - 1), ADD, ADD,
-               ["kS", "kX"], ["kU%d" % k])
-        tt(T.kV[:], T.kU[:], T.kM[:], MUL, km + ["kU%d" % k for k in range(8)], ["kV"])
-        tt(T.kA[:], T.kV[:, 0:2 * LW], T.kV[:, 2 * LW:], ADD, ["kV"], ["kA"])
-        tt(T.kG[:], T.kA[:, 0:LW], T.kA[:, LW:], ADD, ["kA"], ["kG"])
-        ts(T.kL[:, 0:LW], T.kG[:], 15, None, AND, None, ["kG"], ["kL0"])
-        ts(T.kL[:, LW:], T.kG[:], 4, None, SHR, None, ["kG"], ["kL1"])
-        ts(T.kR[:], T.kL[:, 0:LW], float(ROW), None, MUL, None, ["kL0"], ["kR"])
+    def row_order(a, b, reads):
         for k in range(2):
-            tt(T.kD[:, :, 16 * k:16 * k + 16], T.kR[:], T.kL[:, LW:], ADD, ["kR", "kL1"], ["kD%d" % k])
-        op("v", lambda: g.vector.transpose(T.kT[:], T.kD[:]), ["kD0", "kD1"], ["kT"])
+            tt(T.kD[:, :, 16 * k:16 * k + 16], a, b, ADD, reads, ["kD%d" % k])
+        turn(T.kT[:], T.kD[:], ["kD0", "kD1"], ["kT"])
         cp("v", T.oT[:], T.kT[:].indirect(T.oS[:, 0:3]), ["kT", "oS"], ["oT"])
 
-    def place(X, xk):
-        L = [T.hL[:, SW * k:SW * k + SW] for k in range(5)]
-        tt(T.hE[:], X, T.cD[:, 2 * SW:3 * SW], ADD, [xk, "cC"], ["hE"])
-        tt(L[0], T.hE[:], T.cD[:, SW:2 * SW], MAX, ["hE", "cD"], ["hI"])
-        ts(L[1], L[0], 15, None, AND, None, ["hI"], ["hL0"])
-        ts(L[2], L[0], 4, None, SHR, None, ["hI"], ["hL1"])
-        ts(L[3], L[1], float(ROW), None, MUL, None, ["hL0"], ["hR"])
-        tt(L[4], L[3], L[2], ADD, ["hR", "hL1"], ["hT"])
-        cp("v", T.oH[:], L[4], ["hT"], ["oH"])
+    def place(X, xk, width, base):
+        ts(T.hq[:], X, 1.0 / 16, -15.0 / 32, MUL, ADD, [xk], ["hq"])
+        line("sv", T.hb[:], X, float(width), float(base - lo // 16), [xk], ["hb"])
+        ts(T.ha[:], T.hq[:], 1.0 - 16 * width, None, MUL, None, ["hq"], ["ha"])
+        tt(T.hb[:], T.hb[:], T.ch[:], ADD, ["hb", "ch"], ["hb"])
+        tt(T.ha[:], T.ha[:], T.hb[:], ADD, ["ha", "hb"], ["ha"])
+        cp("v", T.oH[:], T.ha[:], ["ha"], ["oH"])
 
-    def layer(m, src, tile, c, b0, es, reads, then=None):
-        a, n = CH[c]
+    def layer(m, src, tile, c, reads, cuts=CH):
+        a, n = cuts[c]
+        b0 = 4 * (c % 2)
         quant(m, a, n, src, reads, ["q%s%d" % (m, c)])
         for b in range(4):
             mm(b0 + b, "W", 128 * b, m, a, n, ["qW", "q%s%d" % (m, c)])
-        if then:
-            then()
         for b in range(4):
-            out, reads, writes = T[tile][:, 4 * a + b:4 * (a + n):4], ["ps%d" % (b0 + b)], ["%s%d%d" % (tile, c, b)]
-            if es[b] == "v":
-                ts(out, bank(b0 + b, n), 0.03125, None, MUL, None, reads, writes)
-            else:
-                act(out, bank(b0 + b, n), 0.0, 0.03125, reads, writes)
+            line("sv", T[tile][:, 4 * a + b:4 * (a + n):4], bank(b0 + b, n), 0.03125, 0.0, ["ps%d" % (b0 + b)], ["%s%d%d" % (tile, c, b)])
 
     def whole(tile):
-        return ["%s%d%d" % (tile, c, b) for c in range(2) for b in range(4)]
+        return ["%s%d%d" % (tile, c, b) for c in range(len(CH)) for b in range(4)]
 
-    def listed(win, width, b, off, n, c):
+    def listed(win, width, b, off, c):
         a, k = CH[c]
-        return win[:, width * b:width * b + width].indirect(off[:, h * n + a // 16:h * n + (a + k) // 16])
+        return win[:, width * b:width * b + width].indirect(off[:, a // 8:(a + k) // 8])
 
-    def products(m, win, width, wkeys, off, okey, gt, gkey, c):
-        a, k = CH[c]
-        for b in range(4):
-            for n in range(2):
-                f = 2 * C * b + C * n + a
-                tt(T["mp"[n] + m][:, 4 * a + b:4 * (a + k):4], listed(win, width, b, off, n, c), gt[:, f:f + k], MUL,
-                   [x % b for x in wkeys] + [okey, "%s%d%d%d" % (gkey, b, n, c)], ["x%s%d%d%d" % (m, b, n, c)])
+    def piece(gt, b, c):
+        return T[gt][:, len(CH) * b + c, :]
 
-    def parts(m, c):
-        return ["x%s%d%d%d" % (m, b, n, c) for b in range(4) for n in range(2)]
+    def gather(gt, win, width, wkeys, off, okey):
+        for c, (a, k) in enumerate(CH):
+            for b in range(4):
+                cp("sv", piece(gt, b, c), listed(win, width, b, off, c), [x % b for x in wkeys] + ["%s%d" % (okey, c)], ["%s%d%d" % (gt, b, c)])
 
-    def mode(m, win, width, wkeys, off, okey, gt, gkey, tile, between, es):
-        e = 4 * CH[1][0]
-        products(m, win, width, wkeys, off, okey, gt, gkey, 0)
-        dma("g", [(T["m" + m][:, 0:e], T["p" + m][:, 0:e])], parts(m, 0), ["y" + m], add=True)
-        between()
-        products(m, win, width, wkeys, off, okey, gt, gkey, 1)
-        if m == "2":
-            layer("M" + m, T["m" + m][:, 0:e], tile, 0, 0, es[0], ["y" + m])
-        tt(T["n" + m][:], T["m" + m][:, e:], T["p" + m][:, e:], ADD, parts(m, 1), ["z" + m])
-        layer("M" + m, T["n" + m][:], tile, 1, 4, es[1], ["z" + m])
-        if m == "1":
-            layer("M" + m, T["m" + m][:, 0:e], tile, 0, 0, es[0], ["y" + m])
+    def mode(m, win, width, wkeys, off, okey, gt, tile):
+        both = T["m" + m]
+        for c, (a, k) in enumerate(CH):
+            for b in range(4):
+                tt(both[:, 8 * a + b:8 * (a + k):4], listed(win, width, b, off, c), piece(gt, b, c), MUL,
+                   [x % b for x in wkeys] + ["%s%d" % (okey, c), "%s%d%d" % (gt, b, c)], ["x%s%d%d" % (m, b, c)])
+            p, q = both[:, 8 * a:8 * a + 4 * k], both[:, 8 * a + 4 * k:8 * (a + k)]
+            dma("g", [(p, q)], ["x%s%d%d" % (m, b, c) for b in range(4)], ["y%s%d" % (m, c)], add=True)
+            layer("M" + m, p, tile, c, ["y%s%d" % (m, c)])
 
-    def store(f, name, a, key, es):
-        dma(es[0], [(T.oc[:, 4 * C * f:4 * C * (f + 1)], u8(T["q" + name][:, a:a + C]))], key, [])
-        dma(es[1], [(T.osc[4 * k:4 * k + 4, C * f:C * (f + 1)], T["s" + name][32 * k:32 * k + 4, a:a + C]) for k in range(4)], key, [])
+    def store(f, name, a, n, key):
+        dma("ysg", [(T.oc[:, 4 * f:4 * (f + n)], u8(T["q" + name][:, a:a + n]))], key, [])
+        for k in range(4):
+            dma("ysg", [(T.osc[4 * k:4 * k + 4, f:f + n], T["s" + name][32 * k:32 * k + 4, a:a + n])], key, [])
+
+    own = [[1, 16], [0, 2], [16, h]]
 
     dma("y", [(T.jw[:], T.jb[:])], [], ["jw"])
     dma("y", [(T.txc[:], T.xc[:])], [], ["txc"])
-    dma("s", [(T.kw[:], T.kc[:])], [], ["kw"])
+    dma("ys", [(T.kw[:], T.kc[:])], [], ["kw"])
+    fill(T.tE[:], 0.0, ["tE"])
     fill(T.one[:], 1.0, ["one"])
-    op("g", lambda: g.affine_select(T.tE[:], T.one[:, 0:516], [[-1, 516]], EQ, 0.0, 3, 4), ["one"], ["tE"])
-    own_columns(T.val1, R, "c1", False)
-    dma("y", [(T.txb[:], T.xb[:])], [], ["txb"])
-    dma("y", rows(T.val1, 1, T.jb) + rows(T.val1, 8, T.kc), ["c10", "c11", "c12"], ["val1"])
-    fill(T.r24[:], 1.0, ["r24"])
-    fill(T.r16[:], 1.0, ["r16"])
-    fill(T.msk[:, 2:3], 0.0, ["msk2"])
-    fill(T.kY[:, 0:32], 0.0, ["kYpad"])
-    fill(T.r24[:, 0:160:h], 0.0, ["r24"])
-    fill(T.r16[:, 0:160:16], 0.0, ["r16"])
-    for k in range(4):
-        fill(T.msk[32 * k:32 * k + 16, 2:3], 1.0, ["msk2"] if k in (0, 3) else [])
-    for row in ("row1", "row3"):
-        for k in range(2):
-            act(T[row][:, 8 * ROW * k:8 * ROW * (k + 1)], T.one[:], EMPTY, 0.0, ["one"], [row + "f%d" % k])
-    act(T.msk[:, 3:4], T.msk[:, 2:3], 1.0, -1.0, ["msk2"], ["msk3"])
-    act(T.tEe[:], T.tE[:], 0.0, T.msk[:, 2:3], ["tE", "msk2"], ["tEe"])
-    act(T.tEo[:], T.tE[:], 0.0, T.msk[:, 3:4], ["tE", "msk3"], ["tEo"])
-
-    sort_a(T.jw[:], "jw")
-    quant("C0", lo, C, T.txc[:], ["txc"], ["qC0%d" % rank])
-    every = list(range(N - 1))
-    remote([(every, eng, u8(T.qC0[:, lo:lo + C]), u8(T.qC0[:, lo:lo + C]))], "aC%d" % rank, ["qC0%d" % rank])
-    remote([(every, eng, T.sC0[:, lo:lo + C], T.sC0[:, lo:lo + C])], "aC%d" % rank, ["qC0%d" % rank])
-    for o in peers:
-        landed("aC%d" % o, 2 * ne, ["qC0%d" % o])
-    cS = ["cS%d" % k for k in range(4)]
-    for k in range(4):
-        iota(T.cS[32 * k:32 * k + 32, 0:3], [[32, 3]], 0, 1, [cS[k]], reads=["tE", "c10", "c11", "c12"])
-    spare.extend([lambda: unit("E", (0,)), lambda: unit("E", (1, 2)), lambda: unit("E", (3,))])
-    sort_b()
-    flush()
-    unpack(0, "C0", lo, C, ["qC0%d" % rank])
-    window("ssss", 0, T.wC, N * C, lo, C, "wC%d" % rank)
-    for b in range(4):
-        cp("s", T.pxb[:, C * b:C * b + C], T.txb[:, b:4 * C:4], ["txb"], ["pxb%d" % b])
-    spare.extend([lambda: None, lambda: None,
-                  lambda: op("v", lambda: g.vector.tensor_reduce(T.msk[:, 4:5], T.tE[:, 35:516:64], AxisListType.X, ADD), ["tE"], ["msk4"]),
-                  lambda: cp("v", T.oK1[:], T.kw[:], ["kw"], ["oK1"]),
-                  lambda: cp("v", T.oS[:, 0:3], T.cS[:, 0:3], cS, ["oS"])])
-    sort_c()
-    cp("v", T.row1[:].indirect(T.oT[:]), T.val1[:], ["oT", "val1", "c10", "c11", "c12", "row1f0", "row1f1"], ["row1"])
-    near = [peers[t] for t in order]
-    dma("y", [(T.lJ[:], T.row1[1:128:16, :])], ["row1"], ["lJ"])
-    dma("y", [(T.lK[:], T.row1[8:128:16, :])], ["row1"], ["lK"])
-    dma("y", [(T.lI[:], T.row1[0:128:16, :])], ["row1"], ["lI"])
-    iota(T.cD[:, 0:SW], [[16, SW]], 0, 1, ["cD0"], reads=cS)
-    iota(T.cD[:, 2 * SW:3 * SW], [[0, N - 1], [C, 2], [0, S // 16]], R - lo, 0, ["cC"])
-    iota(T.pos1[:], [[1, R]], 0, 0, ["pos10"], True)
-    iota(T.tab[:], [[1, N * C]], 0, 0, ["tab0"], True)
-    send_list(T.lJ, T.rJ, "aJ", ["lJ"], "rJ")
-    send_list(T.lK, T.rK, "aK", ["lK"], "rK")
-    own_columns(T.val3, 0, "c3", True)
-    iota(T.pos3[:], [[SL, N - 1], [S - C, 2], [1, S]], 2 * C, 0, ["pos3"], True)
-
-    act(T.msk[:, 5:6], T.msk[:, 4:5], 1.0, -1.0, ["msk4"], ["msk5"])
-    act(T.pos1[:], T.pos1[:], 0.0, T.msk[:, 5:6], ["pos10", "msk5"], ["pos1"])
-    unpack(4, "C0", C * near[0], C, ["qC0%d" % near[0]])
-    window("ssss", 4, T.wC, N * C, C * near[0], C, "wC%d" % near[0])
-    quant("B0", R, C, T.txb[:], ["txb"], ["qB0o"])
-    ts(T.cD[:, 3 * SW:3 * SW + 1], T.cD[:, 0:1], 112, None, AND, None, ["cD0"], ["cp1"])
-    ts(T.u1[:, 0:LW], T.kG[:], float(WN), float(C), AluOpType.is_ge, MUL, ["kG"], ["u1"])
-    cp("v", T.mskD[:, 0:1], T.cD[:, 3 * SW:3 * SW + 1], ["cp1"], ["msk0"])
-    tt(T.u1[:, LW:], T.kG[:], T.u1[:, 0:LW], SUB, ["kG", "u1"], ["u2"])
-    ts(T.cD[:, SW:2 * SW], T.cD[:, 0:SW], T.mskD[:, 0:1], None, SUB, None, ["cD0", "msk0"], ["cD"])
-    cp("v", T.oP1[:], T.u1[:, LW:], ["u2"], ["oP1"])
-    unpack(0, "C0", C * near[1], C, ["qC0%d" % near[1]])
-    window("vvvv", 0, T.wC, N * C, C * near[1], C, "wC%d" % near[1])
-    unpack(4, "C0", C * near[2], C, ["qC0%d" % near[2]])
-    window("ssvs", 4, T.wC, N * C, C * near[2], C, "wC%d" % near[2])
-    unpack(0, "B0", R, C, ["qB0o"])
-    window("vvvv", 0, T.wB, WN, R, C, "wBo")
-    wCk = ["wC%d" % o + "%d" for o in range(N)]
-
-    def gather_c(b):
-        cp("s", T.gC[:, 2 * C * b:2 * C * (b + 1)], T.wC[:, N * C * b:N * C * (b + 1)].indirect(T.oK1[:]),
-           [k % b for k in wCk] + ["oK1"], ["gC%d%d%d" % (b, n, c) for n in range(2) for c in range(2)])
-
-    gather_c(0)
-
-    ts(T.oB0[:], T.rJ[:], float(lo), None, SUB, None, ["rJ"], ["oB0"])
-    for b in (0, 2, 1, 3):
-        cp("vvss"[b], T.cB0[:, b:4 * R:4], T.pxb[:, C * b:C * b + C].indirect(T.oB0[:]), ["pxb%d" % b, "oB0"], ["cB0%d" % b])
-    post(T.cB0, "B0", "aB0")
-    gather_c(1)
-    cp("v", T.oK[:], T.rK[:], ["rK"], ["oK"])
-    act(T.val2[:, R:], T.tab[:].indirect(T.oK[:]), 0.0, T.msk[:, 4:5], ["tab0", "oK", "msk4"], ["hV"])
-    gather_c(2)
-    gather_c(3)
-    spare.extend([lambda t=t: by_element(T.oA, T.lI[:, 0:SW], R, ["lI"], "oA", (t,)) for t in range(4)])
-    place(T.rJ[:], "rJ")
-    flush()
-    tt(T.val2[:, 0:R], T.val2[:, R:], T.pos1[:], ADD, ["hV", "pos1"], ["val2"])
-    cp("v", T.row1[:].indirect(T.oH[:]), T.val2[:, 0:R], ["oH", "val2"], ["row1"])
+    fill(T.c80[:], 80.0, ["c80"])
+    fill(T.kO[:], -1, ["kOg"])
+    scan(T.row1[:, 0:T2], T.c80[:], T.c80[:], -432.0, MIN, SUB, ["c80"], ["row1"])
+    iota(T.zrow[0:4, 3:80:5], [[8, 2], [32, 4], [32 - T2, 2]], T2 - 15, ["z0"])
+    iota(T.zrow[0:4, 83:160:5], [[8, 2], [32, 4], [T2, 2]], 1, ["z1"])
+    iota(T.zrow[0:4, 4:160:5], [[1, 2], [0, 16]], 0, ["z2"])
+    iota(T.srow[0:4], [[16, 2], [1, 16], [32, 3]], 0, ["srow"])
+    note("g", lambda e: g.affine_select(T.tE[:, 3:515:4], T.one[:], [[-1, 128]], EQ, 0.0, 0, 1), ["one"], ["tE"])
+    iota(T.val1[:], own, R, ["val1"], False)
+    iota(T.cK[:], [[S, 6]], 15, ["cK"])
+    for k in range(3):
+        cp("sv", T.zrow[0:4, k:160:5], T.srow[0:4, :, 16 * k:16 * k + 16], ["srow"], ["z%d" % (3 + k)])
+    dma("ys", [(T.cc[:, 0:5], T.zrow[0:4, :])], ["z%d" % k for k in range(6)], ["cc"])
+    dma("ys", [(T.txb[:], T.xb[:])], [], ["txb"])
+    dma("ys", [(T.val1[0:128:16, :], T.jb[:]), (T.val1[1:128:16, :], T.kc[:])], [], ["val1"])
+    line("s", T.rr[:], T.c80[:, 0:6 * G + 32], 0.0, 1.0, ["c80"], ["r25", "r16"])
+    line("s", T.cz[:, 608:736], T.c80[:, 0:128], 0.0, 0.0, ["c80"], ["cz"])
+    line("s", T.rr[:, 0:6 * G:G], T.c80[:, 0:6], 0.0, 0.0, ["c80"], ["r25"])
+    line("s", T.rr[:, 6 * G::16], T.c80[:, 0:2], 0.0, 0.0, ["c80"], ["r16"])
+    line("s", T.kW[:, :, 0:1], T.c80[:, 0:2], 0.0, 0.0, ["c80"], ["kWg"])
+    line("s", T.kU[:, 6 * G::G], T.c80[:, 0:2], 0.0, 0.0, ["c80"], ["kUg"])
+    line("s", T.cc[:, 6:7], T.cc[:, 4:5], -1.0, 1.0, ["cc"], ["ev"])
+    line("s", T.tEe[:], T.tE[:], T.cc[:, 6:7], 0.0, ["tE", "ev"], ["tEe"])
+    line("s", T.tEo[:], T.tE[:], T.cc[:, 4:5], 0.0, ["tE", "cc"], ["tEo"])
+    unit("E")
     unit("Ee")
     unit("Eo")
+
+    quant("C0", lo, C, T.txc[:], ["txc"], ["qC0%d" % rank])
+    every = list(range(N - 1))
+    remote([(every, eng, T.sC0[:, lo:lo + C], T.sC0[:, lo:lo + C])], "aC%d" % rank, ["qC0%d" % rank])
+    remote([(every, eng, u8(T.qC0[:, lo:lo + C]), u8(T.qC0[:, lo:lo + C]))], "aC%d" % rank, ["qC0%d" % rank])
+    came = peers[::-1]
+    for o in came:
+        landed("aC%d" % o, 2 * ne, ["qC0%d" % o])
+    unpack(0, "C0", lo, C, ["qC0%d" % rank])
+    window(0, T.wC, N * C, lo, C, "wC%d" % rank)
+    number(T.jw[:], "jw")
+    ts(T.kq[:], T.jw[:], 4, None, SHR, None, ["jw"], ["kq"])
+    for n in range(2):
+        ts(T.kb[:, h * n:h * n + h], T.jw[:, h * n:h * n + h], float(LW), float(OWN1 - lo // 16 + h * n), MUL, ADD, ["jw"], ["kb%d" % n])
+    ts(T.ka[:], T.kq[:], 1.0 - 16 * LW, None, MUL, None, ["kq"], ["ka"])
+    tt(T.kW[:, :, 1:G], T.ka[:], T.kb[:], ADD, ["ka", "kb0", "kb1", "kWg"], ["kW"])
+    tt(T.kV[:, 6:8, :], T.kW[:], T.kM[:, 6 * G:], MUL, ["kW", "kM3"], ["kVo"])
+    tt(T.kV[:, 0:6, :], T.kU[:, 0:6 * G], T.kM[:, 0:6 * G], MUL, km + ["kU"], ["kV"])
+    cp("v", T.oS[:, 0:3], T.cc[:, 0:3], ["cc"], ["oS"])
+    ts(T.oX[:, 0:3], T.cK[:, 0:6:2], T.cc[:, 3:4], None, ADD, None, ["cK", "cc"], ["oX"])
+    ts(T.u1[:], T.jw[:], float(R + 16 - lo), float(R + 16), ADD, MAX, ["jw"], ["u1"])
+    chunked(T.oK1, T.kw, 0.0, ["kw"], "oK1")
+    tt(T.kA[:], T.kV[:, 0:4, :], T.kV[:, 4:8, :], ADD, ["kV", "kVo"], ["kA"])
+    row_order(T.kA[:, 0:2, 1:G], T.kA[:, 2:4, 1:G], ["kA"])
+    cp("v", T.row1[:].indirect(T.oT[:]), T.val1[:], ["oT", "val1"], ["row1"])
+    dma("ys", [(T.dK[t], T.row1[1:128:16, 16 + SL * t:16 + SL * (t + 1)]) for t in range(N - 1)], ["row1"], ["dK"])
+    turn(T.cz[:, 0:T2], T.row1[:, 0:T2], ["row1"], ["kE0"])
+    turn(T.cz[:, T2:T2 + R], T.row1[:, 16:16 + R], ["row1"], ["kE1"])
+    cp("vs", T.kF[:], T.cz[:, 0:640].indirect(T.oX[:, 0:3]), ["kE0", "kE1", "oX", "cz"], ["kF"])
+    iota(T.val2[:], [[1, R]], 0, ["val2"])
+    iota(T.ch[:], [[0, N - 1], [h, 2], [0, S // 16]], 0, ["ch"])
+    send_list(block(T.kF, 16), block(T.rJ), "aJ", ["kF"], "rJ")
+    send_list(lambda t: T.dK[t], lambda t: T.dL[t], "aK", ["dK"], "dL")
+    dma("ys", [(T.val2[1:128:16, SL * t:SL * (t + 1)], T.dL[t]) for t in range(N - 1)], ["dL"], ["val2"])
+    tt(T.l3[:, 4:6, :], T.kD[:, :, 0:16], T.u1[:], MIN, ["kD0", "u1"], ["u2"])
+    cp("sv", T.kI[:], T.kF[:], ["kF"], ["kI"])
+    chunked(T.oP1, T.l3[:, 4:6, :], -16.0, ["u2"], "oP1")
+
+    quant("B0", R, C, T.txb[:], ["txb"], ["qB0o"])
+    unpack(4, "B0", R, C, ["qB0o"])
+    window(4, T.wB, WN, R, C, "wBo")
+    for k, o in enumerate(came):
+        unpack(4 * (k % 2), "C0", C * o, C, ["qC0%d" % o])
+        window(4 * (k % 2), T.wC, N * C, C * o, C, "wC%d" % o)
+    wCk = ["wC%d" % o + "%d" for o in range(N)]
+    gather("gC", T.wC, N * C, wCk, T.oK1, "oK1")
+
+    by_element(T.oB0, T.rJ[:], lo, ["rJ"], "oB0")
+    compose(T.cB0, T.txb, T.oB0, "B0", ["txb"])
+    post(T.cB0, "B0", "aB0")
+    iota(T.val3[:], own, 0, ["val3"])
+    dma("g", [(T.tv[:], T.v[:])], [], ["tv"])
+    iota(T.row3[:, OWN3:], [[-80 * SW, 16], [-80, ROW]], -16 * S, ["row3"])
+    iota(T.pos3[:], [[SL, N - 1], [S - C, 2], [1, S]], 2 * C, ["pos3"])
+    by_element(T.oA, T.kI[:, :, 8:14], R, ["kI"], "oA")
+    place(T.rJ[:], "rJ", LW, OWN1)
+    cp("v", T.row1[:].indirect(T.oH[:]), T.val2[:], ["oH", "val2"], ["row1"])
+    dma("ys", [(T.lQ[:], T.row1[1:128:16, OWN1:])], ["row1"], ["lQ"])
+    dma("ys", [(T.lP[:], T.row1[8:128:16, OWN1:])], ["row1"], ["lP"])
     unpack(4, "B0", 0, R, ["qB0a"])
-    window("vsvs", 4, T.wB, WN, 0, R, "wBa")
-    dma("y", [(T.lQ[:], T.row1[8:128:16, :])], ["row1"], ["lQ"])
-    dma("y", [(T.lP[:], T.row1[0:128:16, :])], ["row1"], ["lP"])
-    dma("y", [(u8(T.qW[:]), T.wc[:]), (T.sW[:], T.ws[:])], ["qB0a"], ["qW"])
-    dma("y", rows(T.val3, 0, T.lP, SW) + rows(T.val3, 8, T.lQ, SW), ["c30", "c31", "c32", "lP", "lQ"], ["val3"])
-    dma("y", [(T.tv[:], T.v[:])], [], ["tv"])
+    window(4, T.wB, WN, 0, R, "wBa")
+    dma("ys", [(u8(T.qW[:]), T.wc[:]), (T.sW[:], T.ws[:])], [], ["qW"])
+    dma("ys", [(T.val3[0:128:16, :], T.lP[:]), (T.val3[8:128:16, :], T.lQ[:])], ["lP", "lQ"], ["val3"])
+    quant("V", 0, 128, T.tv[:], ["tv"], ["qV"])
 
-    mode("1", T.wB, WN, ["wBo%d", "wBa%d"], T.oP1, "oP1", T.gC, "gC", "tA", lambda: None, ("vvss", "ssss"))
-    compose("ssss", T.cA, T.tA, T.oA, "A", whole("tA"))
-
-    spare.extend([lambda: None, lambda: cp("v", T.oP2[:], T.lP[:, SW:], ["lP"], ["oP2"]), lambda: cp("v", T.oK2[:], T.lQ[:, SW:], ["lQ"], ["oK2"]),
-                  lambda: quant("A", R, C, T.tA[:], whole("tA"), ["qAo"])])
-    sort_a(T.lQ[:, SW:], "lQ")
-    sort_b()
-    flush()
-    unpack(0, "A", R, C, ["qAo"])
+    mode("1", T.wB, WN, ["wBo%d", "wBa%d"], T.oP1, "oP1", "gC", "tA")
+    compose(T.cA, T.tA, T.oA, "A", whole("tA"))
     post(T.cA, "A", "aA")
-    window("ssss", 0, T.wA, WN, R, C, "wAo")
-    sort_c()
-    unpack(4, "A", 0, R, ["qAa"])
-    window("ssss", 4, T.wA, WN, 0, R, "wAa")
-    for c in range(2):
-        for b in range(4):
-            for n in range(2):
-                f = 2 * C * b + C * n + CH[c][0]
-                cp("s", T.gA[:, f:f + CH[c][1]], listed(T.wA, WN, b, T.oP2, n, c), ["wAo%d" % b, "wAa%d" % b, "oP2"], ["gA%d%d%d" % (b, n, c)])
-    cp("v", T.row3[:].indirect(T.oT[:]), T.val3[:], ["oT", "val3", "c30", "c31", "c32", "row3f0", "row3f1"], ["row3"])
-    dma("y", [(T.dupe[0:128:32, :], T.row3[0:128:32, :]), (T.dupe[16:128:32, :], T.row3[0:128:32, :]),
-              (T.dupo[0:128:32, :], T.row3[16:128:32, :]), (T.dupo[16:128:32, :], T.row3[16:128:32, :])], ["row3"], ["dup"])
-    dma("y", [(T.mJ[:], T.row3[3:128:16, :])], ["row3"], ["mJ"])
-    dma("y", [(T.mK[:], T.row3[8:128:16, :])], ["row3"], ["mK"])
-    dma("y", [(T.fE[:], T.dupe[0:128:16, :]), (T.fO[:], T.dupo[0:128:16, :])], ["dup"], ["fEO"])
-    send_list(T.mK, T.rK3, "aK3", ["mK"], "rK3")
-    store(0, "A", R, ["qAo", "qAa"], "yy")
+    quant("A", R, C, T.tA[:], whole("tA"), ["qAo"])
+    unpack(0, "A", R, C, ["qAo"])
+    window(0, T.wA, WN, R, C, "wAo")
 
-    def hand_on():
-        by_element(T.oB1, T.mJ[:, 0:SW], 0, ["mJ"], "oB1")
-        cp("v", T.oF[:, 0:SW], T.fE[:, 0:SW], ["fEO"], ["oF0"])
-        cp("v", T.oF[:, SW:], T.fO[:, 0:SW], ["fEO"], ["oF1"])
-        quant("V", 0, 128, T.tv[:], ["tv"], ["qV"])
-        cp("v", T.qF[:].bitcast(dt.uint32), T.qA[:].bitcast(dt.uint32).indirect(T.oF[:]), ["qAo", "qAa", "oF0", "oF1"], ["qF"])
-        cp("s", T.sF[:], T.sA[:].indirect(T.oF[:]), ["qAo", "qAa", "oF0", "oF1"], ["sF"])
-        six = [(t, p) for t in order for p in range(2)]
-        e8 = ne // 8
-        cut = [eng[e8 * k:e8 * k + e8] for k in range(4)] + [eng[4 * e8:6 * e8], eng[6 * e8:]]
-        for x, f in (("q", u8), ("s", lambda a: a)):
-            remote([([t], es, f(T[x + "F"][:, R * p + SL * t:R * p + SL * t + SL]), f(T[x + "LF"][:, R * p + SL * (N - 2 - t):R * p + SL * (N - 1 - t)]))
-                    for (t, p), es in zip(six, cut)], "aF", [x + "F"])
-        landed("aF", 2 * got, ["qLF"])
-        mm(4, "V", 0, "A", R, C, ["qV", "qAo"])
-        cp("s", T.yt[:, 0:C], bank(4, C), ["ps4"], ["yt0"])
-
-    mode("2", T.wC, N * C, wCk, T.oK2, "oK2", T.gA, "gA", "tB", hand_on, ("ssss", "ssss"))
-    compose("ssss", T.cB1, T.tB, T.oB1, "B1", whole("tB"))
-    place(T.rK3[:], "rK3")
+    number(T.lQ[:], "lQ")
+    for n in range(2):
+        line("sv", T.kU[:, (6 + n) * G + 1:(7 + n) * G], T.lQ[:, h * n:h * n + h], 1.0, float(R + 16 - lo + C * n), ["lQ", "kUg"], ["kUo%d" % n])
+    cp("sv", T.l3[:, 0:2, :], T.lP[:], ["lP"], ["l3P"])
+    cp("sv", T.l3[:, 2:4, :], T.lQ[:], ["lQ"], ["l3Q"])
+    chunked(T.oP2, T.l3[:, 0:2, :], 0.0, ["l3P"], "oP2")
+    chunked(T.oK2, T.l3[:, 2:4, :], 0.0, ["l3Q"], "oK2")
+    tt(T.kV[:], T.kU[:], T.kM[:], MUL, km + ["kU", "kM3", "kUo0", "kUo1"], ["kV", "kVo"])
+    tt(T.kA[:], T.kV[:, 0:4, :], T.kV[:, 4:8, :], ADD, ["kV", "kVo"], ["kA"])
+    tt(T.kG[:], T.kA[:, 0:2, 1:G], T.kA[:, 2:4, 1:G], ADD, ["kA"], ["kG"])
+    ts(T.kq[:], T.kG[:], 4, None, SHR, None, ["kG"], ["kq"])
+    ts(T.kb[:], T.kG[:], float(ROW), float(OWN3 - 1), MUL, ADD, ["kG"], ["kb0", "kb1"])
+    ts(T.ka[:], T.kq[:], 1.0 - 16 * ROW, None, MUL, None, ["kq"], ["ka"])
+    row_order(T.ka[:], T.kb[:], ["ka", "kb0", "kb1"])
+    cp("v", T.row3[:].indirect(T.oT[:]), T.val3[:], ["oT", "val3"], ["row3"])
+    r3 = T.row3[:, OWN3:]
+    dma("ys", [(T.mK[:], r3[8:128:16, :])], ["row3"], ["mK"])
+    dma("ys", [(T.dupe[0:128:32, :], r3[0:128:32, :]), (T.dupe[16:128:32, :], r3[0:128:32, :]),
+               (T.dupo[0:128:32, :], r3[16:128:32, :]), (T.dupo[16:128:32, :], r3[16:128:32, :])], ["row3"], ["dup"])
+    dma("ys", [(T.mJ[:], r3[3:128:16, :])], ["row3"], ["mJ"])
+    dma("ys", [(T.fE[:], T.dupe[0:128:16, :]), (T.fO[:], T.dupo[0:128:16, :])], ["dup"], ["fEO"])
+    send_list(block(T.mK), block(T.rK3), "aK3", ["mK"], "rK3")
+    place(T.rK3[:], "rK3", ROW, OWN3 + SW)
     cp("v", T.row3[:].indirect(T.oH[:]), T.pos3[:], ["oH", "pos3"], ["row3"])
-    dma("y", [(T.mP[:], T.row3[3:128:16, :])], ["row3"], ["mP"])
+    dma("ys", [(T.mP[:], r3[3:128:16, :])], ["row3"], ["mP"])
+    cp("v", T.oP3[:], T.mP[:, SW:], ["mP"], ["oP3"])
+    by_element(T.oB1, T.mJ[:, 0:SW], 0, ["mJ"], "oB1")
+
+    unpack(4, "A", 0, R, ["qAa"])
+    window(4, T.wA, WN, 0, R, "wAa")
+    gather("gA", T.wA, WN, ["wAo%d", "wAa%d"], T.oP2, "oP2")
+    store(0, "A", R, C, ["qAo"])
+    cp("v", T.oF[:, 0:SW], T.fE[:, 0:SW], ["fEO"], ["oF0"])
+    cp("v", T.oF[:, SW:], T.fO[:, 0:SW], ["fEO"], ["oF1"])
+    cp("v", T.qF[:].bitcast(dt.uint32), T.qA[:].bitcast(dt.uint32).indirect(T.oF[:]), ["qAo", "qAa", "oF0", "oF1"], ["qF"])
+    cp("sv", T.sF[:], T.sA[:].indirect(T.oF[:]), ["qAo", "qAa", "oF0", "oF1"], ["sF"])
+    six = [(t, p) for t in order for p in range(2)]
+    e8 = ne // 8
+    cut = [eng[e8 * k:e8 * k + e8] for k in range(4)] + [eng[4 * e8:6 * e8], eng[6 * e8:]]
+    for x, f in (("q", u8), ("s", lambda a: a)):
+        remote([([t], es, f(T[x + "F"][:, R * p + SL * t:R * p + SL * t + SL]), f(T[x + "LF"][:, R * p + SL * (N - 2 - t):R * p + SL * (N - 1 - t)]))
+                for (t, p), es in zip(six, cut)], "aF", [x + "F"])
+    landed("aF", 2 * got, ["qLF"])
+    mm(0, "V", 0, "A", R, C, ["qV", "qAo"])
+    cp("sv", T.yt[:, 0:C], bank(0, C), ["ps0"], ["yt0"])
+    mode("2", T.wC, N * C, wCk, T.oK2, "oK2", "gA", "tB")
+    compose(T.cB1, T.tB, T.oB1, "B1", whole("tB"))
+    post(T.cB1, "B1", "aB1")
     quant("B1", R, C, T.tB[:], whole("tB"), ["qB1o"])
     unpack(0, "B1", R, C, ["qB1o"])
-    post(T.cB1, "B1", "aB1")
-
-    def last(c):
-        a, k = CH[c]
-        quant("C1", a, k, T.tC[:, 4 * a:4 * (a + k)], ["tC%d%d" % (c, b) for b in range(4)], ["qC1%d" % c])
-        mm(c, "V", 0, "C1", a, k, ["qV", "qC1%d" % c])
-        cp("s", T.yt[:, 2 * C + a:2 * C + a + k], bank(c, k), ["ps%d" % c], ["yt2%d" % c])
-        dma("s", [(T.y[:, 2 * C + a:2 * C + a + k], T.yt[:, 2 * C + a:2 * C + a + k])], ["yt2%d" % c], [])
 
     for b in range(4):
         for n in range(2):
             a = W3 * b + C * n
-            f = 2 * C * b + C * n
-            tt(T.w3[:, a:a + C], bank(b, C), T.gA[:, f:f + C], MUL, ["ps%d" % b, "gA%d%d0" % (b, n), "gA%d%d1" % (b, n)], ["w3%d%d" % (n, b)])
+            tt(T.w3[:, a:a + C], bank(b, C), T.gA[:, 2 * b:2 * b + 2, C // 2 * n:C // 2 * (n + 1)], MUL,
+               ["ps%d" % b] + ["gA%d%d" % (b, c) for c in range(2)], ["w3%d%d" % (n, b)])
     for b in range(4):
         mm(4 + b, "Ee", 128 * b, "LF", 0, R, ["qEe%d" % b, "qLF"], True, False)
         mm(4 + b, "Eo", 128 * b, "LF", R, R, ["qEo%d" % b, "qLF"], False, True)
-    window("ssss", 4, T.fA, R, 0, R, "fA")
+    window(4, T.fA, R, 0, R, "fA")
     mm(0, "V", 0, "B1", R, C, ["qV", "qB1o"])
-    cp("s", T.yt[:, C:2 * C], bank(0, C), ["ps0"], ["yt1"])
+    cp("sv", T.yt[:, C:2 * C], bank(0, C), ["ps0"], ["yt1"])
     unpack(4, "B1", 0, R, ["qB1a"])
-    dma("y", [(T.y[:, 0:2 * C], T.yt[:, 0:2 * C])], ["yt0", "yt1", "qB1a"], [])
-    store(1, "B1", R, ["qB1o", "qB1a"], "yy")
-    for n in range(2):
-        ts(T.oP3[:, h * n:h * n + h], T.mP[:, SW + h * n:SW + h * n + h], float(C * n), None, ADD, None, ["mP"], ["oP3%d" % n])
+    dma("ys", [(T.y[:, 0:2 * C], T.yt[:, 0:2 * C])], ["yt0", "yt1"], [])
+    store(C, "B1", R, C, ["qB1o"])
     for b in range(4):
         tt(T.w3[:, W3 * b + 2 * C:W3 * (b + 1)], bank(4 + b, R), T.fA[:, R * b:R * b + R], MUL, ["ps%d" % (4 + b), "fA%d" % b], ["w3a%d" % b])
-    for c in range(2):
-        a, k = CH[c]
-        for b in range(4):
-            cp("s", T.g3[:, C * b + a:C * b + a + k], listed(T.w3, W3, b, T.oP3, 0, c),
-               ["w30%d" % b, "w31%d" % b, "w3a%d" % b, "oP30"], ["g3%d%d" % (c, b)])
-    for c in range(2):
-        a, k = CH[c]
-        for b in range(4):
-            tt(T.m3[:, 4 * a + b:4 * (a + k):4], listed(T.w3, W3, b, T.oP3, 1, c), T.g3[:, C * b + a:C * b + a + k], ADD,
-               ["w30%d" % b, "w31%d" % b, "w3a%d" % b, "oP31", "g3%d%d" % (c, b)], ["M3%d%d" % (c, b)])
-        layer("M3", T.m3[:, 4 * a:4 * (a + k)], "tC", c, 4 * c, ("ssss", "vvvv")[c], ["M3%d%d" % (c, b) for b in range(4)],
-              (None, lambda: last(0))[c])
-    last(1)
-    store(2, "C1", 0, ["qC10", "qC11"], "yy")
 
-    need("y", list(total.items()))
+    def half(b, n, c):
+        a, k = CH3[c]
+        return T.w3[:, W3 * b + C * n:W3 * (b + 1)].indirect(T.oP3[:, h * n + a // 16:h * n + (a + k) // 16])
+
+    for c, (a, k) in enumerate(CH3):
+        for b in range(4):
+            slots = ["w3a%d" % b, "oP3"]
+            cp("sv", T.g3[:, C * b + a:C * b + a + k], half(b, 0, c), ["w30%d" % b, "w31%d" % b] + slots, ["g3%d%d" % (c, b)])
+            tt(T.m3[:, 4 * a + b:4 * (a + k):4], half(b, 1, c), T.g3[:, C * b + a:C * b + a + k], ADD,
+               ["w31%d" % b] + slots + ["g3%d%d" % (c, b)], ["M3%d%d" % (c, b)])
+        layer("M3", T.m3[:, 4 * a:4 * (a + k)], "tC", c, ["M3%d%d" % (c, b) for b in range(4)], CH3)
+    for c, (a, k) in enumerate(CH3):
+        quant("C1", a, k, T.tC[:, 4 * a:4 * (a + k)], ["tC%d%d" % (c, b) for b in range(4)], ["qC1%d" % c])
+        mm(c, "V", 0, "C1", a, k, ["qV", "qC1%d" % c])
+        cp("sv", T.yt[:, 2 * C + a:2 * C + a + k], bank(c, k), ["ps%d" % c], ["yt2%d" % c])
+        dma("ys", [(T.y[:, 2 * C + a:2 * C + a + k], T.yt[:, 2 * C + a:2 * C + a + k])], ["yt2%d" % c], [])
+        store(2 * C + a, "C1", a, k, ["qC1%d" % c])
+
+    issue()

from concourse.bass import DstId, RemoteDMATransfer
from concourse.mybir import dt, AluOpType, ActivationFunctionType

N = 4
C = 384
S = 48
SL = 2 * S
R = (N - 1) * SL
CH = ((0, 192), (192, 192))
CH3 = ((0, 256), (256, 128))
LW = 2 * C // 16
h = LW // 2
SW = R // 16
ROW = SW + LW
WN = R + C
W3 = 2 * C + R
G = h + 1
OWN1 = 2048
OWN3 = 1808
T2 = R + 32

X4, U8, BF, F32, I32, U16 = "float8_e4m3fn_x4", "uint8", "bfloat16", "float32", "int32", "uint16"
SCRATCH = {"ps": ("psum", [128, 4096], F32), "dK": ("dram", [N - 1, 128, SL // 16], F32), "dL": ("dram", [N - 1, 128, SL // 16], F32)}


def _sb(dtype, **kw):
    for name, n in kw.items():
        SCRATCH[name] = ("sbuf", [128] + (list(n) if isinstance(n, tuple) else [n]), dtype)


_PAIRS = dict(W=512, V=128, E=512, Ee=512, Eo=512, C0=N * C, B0=WN, A=WN, B1=WN, C1=C, M1=C, M2=C, M3=C,
              sB0=R, sA=R, sB1=R, F=2 * R, LF=2 * R)
_sb(X4, **{"q" + k: n for k, n in _PAIRS.items()})
_sb(U8, **{"s" + k: n for k, n in _PAIRS.items()})
_sb(BF, txb=4 * C, txc=4 * C, tv=512, tE=516, tEe=516, tEo=516, one=128, c80=T2, wC=4 * N * C, wB=4 * WN, wA=4 * WN, w3=4 * W3,
    gC=(8, C), gA=(8, C), g3=4 * C, m1=8 * C, m2=8 * C, fA=4 * R, m3=4 * C,
    tA=4 * C, tB=4 * C, tC=4 * C, cB0=4 * R, cA=4 * R, cB1=4 * R)
_sb(F32, yt=3 * C, row1=OWN1 + 2 * C, row3=OWN3 + 16 * ROW, val2=R, val3=2 * C, pos3=R, rr=6 * G + 32, cz=736, zrow=160, srow=(2, LW), cc=8,
    cK=6, ch=SW, kM=8 * G, kS=6 * G, kU=8 * G, kV=(8, G), kA=(4, G), kW=(2, G), kD=(3, 32), kZ=64, kT=96, kF=48, kI=(3, 16), ka=LW, kb=LW,
    rJ=SW, lP=LW, lQ=LW, l3=(6, h), mJ=ROW, mK=ROW, rK3=SW, mP=ROW, dupe=16 * ROW, dupo=16 * ROW, fE=ROW, fO=ROW, u1=LW, ha=SW, hb=SW)
_sb(I32, jw=LW, kw=(2, h), val1=2 * C, kO=(2, G), kG=LW, kq=LW, hq=SW)
_sb(U16, oS=4, oX=4, oT=LW, oH=SW, oK1=LW, oP1=LW, oP2=LW, oK2=LW, oP3=LW, oB0=4 * SW, oA=4 * SW, oB1=4 * SW, oF=2 * SW)

SEMAPHORES = (["cv", "cs", "ct", "cg", "sent", "aJ", "aK", "aK3", "aB0", "aA", "aB1", "aF"]
              + ["aC%d" % k for k in range(N)] + ["d%d" % k for k in range(64)])

ADD, SUB, MUL, MAX, MIN = AluOpType.add, AluOpType.subtract, AluOpType.mult, AluOpType.max, AluOpType.min
EQ, SHR = AluOpType.is_equal, AluOpType.arith_shift_right
COPY, IDENT = ActivationFunctionType.Copy, ActivationFunctionType.Identity

PLAN = (
    "0 11 3 1 4 5 19y 16s 12 6 15s 7 25 21 8 31 10 17s 32 9 26 30 24 14 56 23 18y 68 13 59 22 2y 57 58 69 70 61 42 62s 27 60 29 63 50 33 64 101 43 54s 20y "
    "65 71 102 179y 66 28 103 72 49 44 67 155 104 73 48 74 51 106s 105 80 107s 82 81 75 53s 83 76 84 45 77 52s 85 46 108s 110 47 119 112 109s 111 118 55s "
    "114s 113 120 115s 126 116s 122s 128 121 86y 88 124s 87 117s 89v 40 92 98v 90 97 129 123v 127 93 100 99 91 181 94 161 145 143 142 149s 144 147v 95 "
    "96y 148s 146v 163v 132s 150 162 130s 79 151 78 152 37 154 38 133s 164 160 165 39 166 136s 41 153 167 171 134v 125s 168 156 138s 174 173 172 137s "
    "131s 175v 169y 170y 182 178s 177s 196 176s 180y 185 135s 184 139s 183 141s 197 186 140s 199 240s 198 239s 227 158 200 228 229 230 232 157 35 233s 34 "
    "242s 234 241s 235 187 236 191 189 237 188 231 190 244 192s 238 36 195s 247 193s 201 194s 248 205 204 246 202 209s 203 208v 206s 207v 249 210s 218 "
    "250 213s 159 294y 220 252 221 251 296y 212v 219 211s 222 253 254 223s 214 255 245 215 305 216 256 243 306s 257 293s 295s 217 225s 280 277 279 278 "
    "226s 224s 284s 283s 282s 286s 281v 258y 260y 285v 287s 259y 288s 307 262 308 289s 263 309 261y 290s 297y 310 291s 321 311 292s 322 265s 323 324 298 "
    "299 325 264 267 301s 312 266 274 313 275 314 268 316 315 300 318s 303 319s 269 320s 276 302 273 326 317s 270 328 327 330 332s 329 331s 334s 304 333v "
    "271y 343 338s 335v 336s 344 378y 345 379y 347 348 337s 356 360 361 358 349 357 376s 362 363 375s 359 339 346 366s 368 350 340 377s 341 364s 351 367s "
    "354 342 365s 355 369s 272 371 352 370 372 373 374s 353 381 380 386s 382 384s 383 387 388s 385 390s 389 401s 391 407s 402 405s 392 403s 406 394 408 "
    "393 396 398s 395 404 397s 409 400v 413 399s 410 412 411 417v 414s 418 416s 415v 426y 419 422s 427 424y 423s 420v 431y 432s 428 429v 425s 421y 435s "
    "430y 434s 433y"
)


def rank_program(g, core, T, topo):
    rank = T.rank_of(core)
    if rank is None:
        return
    lo = C * rank
    peers = [(rank + 1 + t) % N for t in range(N - 1)]
    pcore = [T.cores[o] for o in peers]
    Q = {"v": g.vector, "s": g.scalar, "t": g.tensor, "g": g, "y": g.sync}
    steps, writer, readers, count = [], {}, {}, {"sent": 0, "dma": 0}

    def note(es, call, reads, writes, more=False, sem=None):
        me, before = len(steps), {}
        for k in reads:
            before[writer[k]] = True
        for k in writes:
            if k in writer:
                before[writer[k]] = before.get(writer[k], False) or not more
            for x in readers.get(k, []):
                before[x] = True
        for k in reads:
            if k.startswith("ps"):
                for x in readers.get(k, []):
                    before.setdefault(x, False)
            readers.setdefault(k, []).append(me)
        for k in writes:
            writer[k], readers[k] = me, []
        steps.append(dict(es=es, call=call, before=before, sem=sem))

    def dma(es, moves, reads, writes, add=False):
        s = "d%d" % count["dma"]
        count["dma"] += 1

        def call(e):
            for out, src in moves:
                (g.dma_start(out, src, accum_op=ADD) if add else Q[e].dma_start(out, src)).then_inc(T.sem[s], 16)
        note(es, call, reads, writes, sem=(s, 16 * len(moves)))

    def remote(moves, sem, reads):
        ts_ = []
        for ts, es, src, dst in moves:
            ids = [DstId(rid=topo.addr(pcore[t])[0], pnc=topo.addr(pcore[t])[1]) for t in ts]
            ts_.append(RemoteDMATransfer(dst_ids=ids, dma_engine_mask=sum(1 << x for x in es), remote_sem=T.sem[sem],
                                         srcs=[src], dsts=[dst] * len(ts)))
            count["sent"] += len(es)
        note("g", lambda e: g.remote_dma_fused(ts_, local_sem=T.sem.sent), reads, [], sem=("sent", 0))

    def landed(sem, n, keys):
        note("", None, [], keys, sem=(sem, n))

    def issue():
        total, waited = {"sent": count["sent"]}, {}
        for w in PLAN.split() or [str(k) for k in range(len(steps))]:
            s = steps[int(w.rstrip("vsyg"))]
            e = s["e"] = s["es"][:1] if w[-1].isdigit() else w[-1]
            if s["sem"] is None:
                total["c" + e] = total.get("c" + e, 0) + 1
                s["tok"] = ("c" + e, total["c" + e])
            elif s["sem"][1]:
                s["tok"] = s["sem"]
                total[s["sem"][0]] = s["sem"][1]
            if not e:
                continue
            top = {}
            for x, hard in s["before"].items():
                if hard or steps[x]["e"] != e:
                    name, v = steps[x]["tok"]
                    top[name] = max(top.get(name, 0), v)
            for name, v in top.items():
                if waited.get((e, name), 0) < v:
                    Q[e].wait_ge(T.sem[name], v)
                    waited[(e, name)] = v
            done = s["call"](e)
            if s["sem"] is None:
                done.then_inc(T.sem[s["tok"][0]], 1)
        for name, v in total.items():
            g.sync.wait_ge(T.sem[name], v)

    eng = [x for x in topo.engines(core, pcore[0]) if all(x in topo.engines(core, c) for c in pcore)]
    ne = len(eng)
    order = sorted(range(N - 1), key=lambda t: topo.die(pcore[t]) != topo.die(core))
    qt = ne // 4
    wide = dict(zip(order, (eng[:qt], eng[qt:2 * qt], eng[2 * qt:])))
    thin = dict(zip(order, (eng[2 * qt:3 * qt], eng[3 * qt:], eng[:2 * qt])))

    def share(src, dst):
        r = T.cores.index(src)
        ps = [T.cores[(r + 1 + t) % N] for t in range(N - 1)]
        o = sorted(range(N - 1), key=lambda t: topo.die(ps[t]) != topo.die(src))
        return 2 * qt if ps[o[-1]] == dst else qt

    got = sum(share(c, core) for c in pcore)

    def u8(ap):
        return ap.bitcast(dt.uint8)

    def send_list(src, dst, sem, reads, key):
        remote([([t], wide[t], src(t), dst(N - 2 - t)) for t in range(N - 1)], sem, reads)
        landed(sem, got, [key])

    def block(buf, step=SL // 16):
        return lambda t: buf[:, step * t:step * t + SL // 16]

    def send_slots(src, dst, sem, reads, key):
        at = [(t, SL * t, SL * (N - 2 - t)) for t in range(N - 1)]
        remote([([t], wide[t], u8(T["q" + src][:, a:a + SL]), u8(T["q" + dst][:, b:b + SL])) for t, a, b in at], sem, reads)
        remote([([t], thin[t], T["s" + src][:, a:a + SL], T["s" + dst][:, b:b + SL]) for t, a, b in at], sem, reads)
        landed(sem, 2 * got, [key])

    def ts(out, src, s1, s2, o0, o1, reads, writes):
        if o1 is None:
            note("v", lambda e: g.vector.tensor_scalar(out, src, s1, None, o0), reads, writes)
        else:
            note("v", lambda e: g.vector.tensor_scalar(out, src, s1, s2, o0, o1), reads, writes)

    def tt(out, a, b, o, reads, writes):
        note("v", lambda e: g.vector.tensor_tensor(out, a, b, o), reads, writes)

    def cp(es, out, src, reads, writes):
        note(es, lambda e: g.vector.tensor_copy(out, src) if e == "v" else g.scalar.activation(out, src, COPY), reads, writes)

    def line(es, out, src, by, plus, reads, writes):
        def call(e):
            if e == "s":
                return g.scalar.activation(out, src, IDENT, bias=plus, scale=by)
            if plus == 0.0:
                return g.vector.tensor_scalar(out, src, by, None, MUL)
            return g.vector.tensor_scalar(out, src, by, plus, MUL, ADD)
        note(es, call, reads, writes)

    def fill(ap, v, writes):
        note("v", lambda e: g.vector.memset(ap, v), [], writes)

    def scan(out, a, b, first, o0, o1, reads, writes):
        note("v", lambda e: g.vector.tensor_tensor_scan(out, a, b, first, o0, o1), reads, writes)

    def turn(out, src, reads, writes):
        note("v", lambda e: g.vector.transpose(out, src), reads, writes)

    def quant(name, a, n, tile, reads, writes):
        note("v", lambda e: g.vector.quantize_mx(T["q" + name][:, a:a + n], T["s" + name][:, a:a + n], tile), reads, writes)

    def mm(bank, w, wa, x, a, n, reads, start=True, stop=True):
        note("t", lambda e: g.tensor.matmul_mx(T.ps[:, 512 * bank:512 * bank + n], T["q" + w][:, wa:wa + 128], T["s" + w][:, wa:wa + 128],
                                               T["q" + x][:, a:a + n], T["s" + x][:, a:a + n], start, stop),
             reads, ["ps%d" % bank], more=not start)

    def bank(k, n):
        return T.ps[:, 512 * k:512 * k + n]

    def unpack(b0, x, a, n, reads):
        for b in range(4):
            mm(b0 + b, "E", 128 * b, x, a, n, ["qE%d" % b] + reads)

    def window(b0, win, width, a, n, key):
        for b in range(4):
            cp("sv", win[:, width * b + a:width * b + a + n], bank(b0 + b, n), ["ps%d" % (b0 + b)], ["%s%d" % (key, b)])

    def iota(ap, pattern, base, writes, small=True):
        if small:
            note("g", lambda e: g.iota(ap, pattern, base, 0, allow_small_or_imprecise_dtypes=True), [], writes)
        else:
            note("g", lambda e: g.iota(ap, pattern, base, 0), [], writes)

    def unit(name):
        for b in range(4):
            quant(name, 128 * b, 128, T["t" + name][:, 3 - b:515 - b], ["t" + name], ["q%s%d" % (name, b)])

    def by_element(out, src, base, reads, key):
        for t in range(4):
            ts(out[:, SW * t:SW * t + SW], src, 4.0, float(t - 4 * base), MUL, ADD, reads, ["%s%d" % (key, t)])

    def compose(tile, src, off, name, reads):
        for t in range(4):
            cp("sv", tile[:, t:4 * R:4], src[:, 0:4 * C].indirect(off[:, SW * t:SW * t + SW]), reads + ["o%s%d" % (name, t)], ["c%s%d" % (name, t)])

    def post(tile, name, sem):
        quant("s" + name, 0, R, tile[:], ["c%s%d" % (name, t) for t in range(4)], ["qs" + name])
        send_slots("s" + name, name, sem, ["qs" + name], "q%sa" % name)

    def chunked(out, src, add, reads, key):
        for c, (a, k) in enumerate(CH):
            ts(out[:, a // 8:(a + k) // 8], src[:, :, a // 16:(a + k) // 16], add, None, ADD, None, reads, ["%s%d" % (key, c)])

    km = ["kM%d" % t for t in range(N - 1)]

    def number(X, xk):
        ts(T.kO[:, :, 1:G], X, 1.0 / C, 0.5 / C - 0.5, MUL, ADD, [xk, "kOg"], ["kO"])
        for t, o in enumerate(peers + [rank]):
            ts(T.kM[:, 2 * G * t:2 * G * (t + 1)], T.kO[:], float(o), None, EQ, None, ["kO"], ["kM%d" % t])
        scan(T.kS[:], T.rr[:, 0:6 * G], T.kM[:, 0:6 * G], 0.0, MUL, ADD, km + ["r25"], ["kS"])
        cp("vs", T.cz[:, 704:710], T.kS[:, h:6 * G:G], ["kS", "cz"], ["kP"])
        turn(T.cz[:, 672:704], T.cz[:, 704:736], ["kP"], ["kY"])
        scan(T.kZ[:, 0:32], T.cz[:, 671:703], T.rr[:, 6 * G:], 0.0, ADD, MUL, ["kY", "r16"], ["kZ"])
        turn(T.kZ[:, 32:64], T.kZ[:, 0:32], ["kZ"], ["kX"])
        tt(T.kM[:, 0:6 * G:G], T.kZ[:, 32:38], T.cK[:], ADD, ["kX", "cK"], km)
        scan(T.kU[:, 0:6 * G], T.rr[:, 0:6 * G], T.kM[:, 0:6 * G], 0.0, MUL, ADD, km, ["kU"])

    def row_order(a, b, reads):
        for k in range(2):
            tt(T.kD[:, :, 16 * k:16 * k + 16], a, b, ADD, reads, ["kD%d" % k])
        turn(T.kT[:], T.kD[:], ["kD0", "kD1"], ["kT"])
        cp("v", T.oT[:], T.kT[:].indirect(T.oS[:, 0:3]), ["kT", "oS"], ["oT"])

    def place(X, xk, width, base):
        ts(T.hq[:], X, 1.0 / 16, -15.0 / 32, MUL, ADD, [xk], ["hq"])
        line("sv", T.hb[:], X, float(width), float(base - lo // 16), [xk], ["hb"])
        ts(T.ha[:], T.hq[:], 1.0 - 16 * width, None, MUL, None, ["hq"], ["ha"])
        tt(T.hb[:], T.hb[:], T.ch[:], ADD, ["hb", "ch"], ["hb"])
        tt(T.ha[:], T.ha[:], T.hb[:], ADD, ["ha", "hb"], ["ha"])
        cp("v", T.oH[:], T.ha[:], ["ha"], ["oH"])

    def layer(m, src, tile, c, reads, cuts=CH):
        a, n = cuts[c]
        b0 = 4 * (c % 2)
        quant(m, a, n, src, reads, ["q%s%d" % (m, c)])
        for b in range(4):
            mm(b0 + b, "W", 128 * b, m, a, n, ["qW", "q%s%d" % (m, c)])
        for b in range(4):
            line("sv", T[tile][:, 4 * a + b:4 * (a + n):4], bank(b0 + b, n), 0.03125, 0.0, ["ps%d" % (b0 + b)], ["%s%d%d" % (tile, c, b)])

    def whole(tile):
        return ["%s%d%d" % (tile, c, b) for c in range(len(CH)) for b in range(4)]

    def listed(win, width, b, off, c):
        a, k = CH[c]
        return win[:, width * b:width * b + width].indirect(off[:, a // 8:(a + k) // 8])

    def piece(gt, b, c):
        return T[gt][:, len(CH) * b + c, :]

    def gather(gt, win, width, wkeys, off, okey):
        for c, (a, k) in enumerate(CH):
            for b in range(4):
                cp("sv", piece(gt, b, c), listed(win, width, b, off, c), [x % b for x in wkeys] + ["%s%d" % (okey, c)], ["%s%d%d" % (gt, b, c)])

    def mode(m, win, width, wkeys, off, okey, gt, tile):
        both = T["m" + m]
        for c, (a, k) in enumerate(CH):
            for b in range(4):
                tt(both[:, 8 * a + b:8 * (a + k):4], listed(win, width, b, off, c), piece(gt, b, c), MUL,
                   [x % b for x in wkeys] + ["%s%d" % (okey, c), "%s%d%d" % (gt, b, c)], ["x%s%d%d" % (m, b, c)])
            p, q = both[:, 8 * a:8 * a + 4 * k], both[:, 8 * a + 4 * k:8 * (a + k)]
            dma("g", [(p, q)], ["x%s%d%d" % (m, b, c) for b in range(4)], ["y%s%d" % (m, c)], add=True)
            layer("M" + m, p, tile, c, ["y%s%d" % (m, c)])

    def store(f, name, a, n, key):
        dma("ysg", [(T.oc[:, 4 * f:4 * (f + n)], u8(T["q" + name][:, a:a + n]))], key, [])
        for k in range(4):
            dma("ysg", [(T.osc[4 * k:4 * k + 4, f:f + n], T["s" + name][32 * k:32 * k + 4, a:a + n])], key, [])

    own = [[1, 16], [0, 2], [16, h]]

    dma("y", [(T.jw[:], T.jb[:])], [], ["jw"])
    dma("y", [(T.txc[:], T.xc[:])], [], ["txc"])
    dma("ys", [(T.kw[:], T.kc[:])], [], ["kw"])
    fill(T.tE[:], 0.0, ["tE"])
    fill(T.one[:], 1.0, ["one"])
    fill(T.c80[:], 80.0, ["c80"])
    fill(T.kO[:], -1, ["kOg"])
    scan(T.row1[:, 0:T2], T.c80[:], T.c80[:], -432.0, MIN, SUB, ["c80"], ["row1"])
    iota(T.zrow[0:4, 3:80:5], [[8, 2], [32, 4], [32 - T2, 2]], T2 - 15, ["z0"])
    iota(T.zrow[0:4, 83:160:5], [[8, 2], [32, 4], [T2, 2]], 1, ["z1"])
    iota(T.zrow[0:4, 4:160:5], [[1, 2], [0, 16]], 0, ["z2"])
    iota(T.srow[0:4], [[16, 2], [1, 16], [32, 3]], 0, ["srow"])
    note("g", lambda e: g.affine_select(T.tE[:, 3:515:4], T.one[:], [[-1, 128]], EQ, 0.0, 0, 1), ["one"], ["tE"])
    iota(T.val1[:], own, R, ["val1"], False)
    iota(T.cK[:], [[S, 6]], 15, ["cK"])
    for k in range(3):
        cp("sv", T.zrow[0:4, k:160:5], T.srow[0:4, :, 16 * k:16 * k + 16], ["srow"], ["z%d" % (3 + k)])
    dma("ys", [(T.cc[:, 0:5], T.zrow[0:4, :])], ["z%d" % k for k in range(6)], ["cc"])
    dma("ys", [(T.txb[:], T.xb[:])], [], ["txb"])
    dma("ys", [(T.val1[0:128:16, :], T.jb[:]), (T.val1[1:128:16, :], T.kc[:])], [], ["val1"])
    line("s", T.rr[:], T.c80[:, 0:6 * G + 32], 0.0, 1.0, ["c80"], ["r25", "r16"])
    line("s", T.cz[:, 608:736], T.c80[:, 0:128], 0.0, 0.0, ["c80"], ["cz"])
    line("s", T.rr[:, 0:6 * G:G], T.c80[:, 0:6], 0.0, 0.0, ["c80"], ["r25"])
    line("s", T.rr[:, 6 * G::16], T.c80[:, 0:2], 0.0, 0.0, ["c80"], ["r16"])
    line("s", T.kW[:, :, 0:1], T.c80[:, 0:2], 0.0, 0.0, ["c80"], ["kWg"])
    line("s", T.kU[:, 6 * G::G], T.c80[:, 0:2], 0.0, 0.0, ["c80"], ["kUg"])
    line("s", T.cc[:, 6:7], T.cc[:, 4:5], -1.0, 1.0, ["cc"], ["ev"])
    line("s", T.tEe[:], T.tE[:], T.cc[:, 6:7], 0.0, ["tE", "ev"], ["tEe"])
    line("s", T.tEo[:], T.tE[:], T.cc[:, 4:5], 0.0, ["tE", "cc"], ["tEo"])
    unit("E")
    unit("Ee")
    unit("Eo")

    quant("C0", lo, C, T.txc[:], ["txc"], ["qC0%d" % rank])
    every = list(range(N - 1))
    remote([(every, eng, T.sC0[:, lo:lo + C], T.sC0[:, lo:lo + C])], "aC%d" % rank, ["qC0%d" % rank])
    remote([(every, eng, u8(T.qC0[:, lo:lo + C]), u8(T.qC0[:, lo:lo + C]))], "aC%d" % rank, ["qC0%d" % rank])
    came = peers[::-1]
    for o in came:
        landed("aC%d" % o, 2 * ne, ["qC0%d" % o])
    unpack(0, "C0", lo, C, ["qC0%d" % rank])
    window(0, T.wC, N * C, lo, C, "wC%d" % rank)
    number(T.jw[:], "jw")
    ts(T.kq[:], T.jw[:], 4, None, SHR, None, ["jw"], ["kq"])
    for n in range(2):
        ts(T.kb[:, h * n:h * n + h], T.jw[:, h * n:h * n + h], float(LW), float(OWN1 - lo // 16 + h * n), MUL, ADD, ["jw"], ["kb%d" % n])
    ts(T.ka[:], T.kq[:], 1.0 - 16 * LW, None, MUL, None, ["kq"], ["ka"])
    tt(T.kW[:, :, 1:G], T.ka[:], T.kb[:], ADD, ["ka", "kb0", "kb1", "kWg"], ["kW"])
    tt(T.kV[:, 6:8, :], T.kW[:], T.kM[:, 6 * G:], MUL, ["kW", "kM3"], ["kVo"])
    tt(T.kV[:, 0:6, :], T.kU[:, 0:6 * G], T.kM[:, 0:6 * G], MUL, km + ["kU"], ["kV"])
    cp("v", T.oS[:, 0:3], T.cc[:, 0:3], ["cc"], ["oS"])
    ts(T.oX[:, 0:3], T.cK[:, 0:6:2], T.cc[:, 3:4], None, ADD, None, ["cK", "cc"], ["oX"])
    ts(T.u1[:], T.jw[:], float(R + 16 - lo), float(R + 16), ADD, MAX, ["jw"], ["u1"])
    chunked(T.oK1, T.kw, 0.0, ["kw"], "oK1")
    tt(T.kA[:], T.kV[:, 0:4, :], T.kV[:, 4:8, :], ADD, ["kV", "kVo"], ["kA"])
    row_order(T.kA[:, 0:2, 1:G], T.kA[:, 2:4, 1:G], ["kA"])
    cp("v", T.row1[:].indirect(T.oT[:]), T.val1[:], ["oT", "val1"], ["row1"])
    dma("ys", [(T.dK[t], T.row1[1:128:16, 16 + SL * t:16 + SL * (t + 1)]) for t in range(N - 1)], ["row1"], ["dK"])
    turn(T.cz[:, 0:T2], T.row1[:, 0:T2], ["row1"], ["kE0"])
    turn(T.cz[:, T2:T2 + R], T.row1[:, 16:16 + R], ["row1"], ["kE1"])
    cp("vs", T.kF[:], T.cz[:, 0:640].indirect(T.oX[:, 0:3]), ["kE0", "kE1", "oX", "cz"], ["kF"])
    iota(T.val2[:], [[1, R]], 0, ["val2"])
    iota(T.ch[:], [[0, N - 1], [h, 2], [0, S // 16]], 0, ["ch"])
    send_list(block(T.kF, 16), block(T.rJ), "aJ", ["kF"], "rJ")
    send_list(lambda t: T.dK[t], lambda t: T.dL[t], "aK", ["dK"], "dL")
    dma("ys", [(T.val2[1:128:16, SL * t:SL * (t + 1)], T.dL[t]) for t in range(N - 1)], ["dL"], ["val2"])
    tt(T.l3[:, 4:6, :], T.kD[:, :, 0:16], T.u1[:], MIN, ["kD0", "u1"], ["u2"])
    cp("sv", T.kI[:], T.kF[:], ["kF"], ["kI"])
    chunked(T.oP1, T.l3[:, 4:6, :], -16.0, ["u2"], "oP1")

    quant("B0", R, C, T.txb[:], ["txb"], ["qB0o"])
    unpack(4, "B0", R, C, ["qB0o"])
    window(4, T.wB, WN, R, C, "wBo")
    for k, o in enumerate(came):
        unpack(4 * (k % 2), "C0", C * o, C, ["qC0%d" % o])
        window(4 * (k % 2), T.wC, N * C, C * o, C, "wC%d" % o)
    wCk = ["wC%d" % o + "%d" for o in range(N)]
    gather("gC", T.wC, N * C, wCk, T.oK1, "oK1")

    by_element(T.oB0, T.rJ[:], lo, ["rJ"], "oB0")
    compose(T.cB0, T.txb, T.oB0, "B0", ["txb"])
    post(T.cB0, "B0", "aB0")
    iota(T.val3[:], own, 0, ["val3"])
    dma("g", [(T.tv[:], T.v[:])], [], ["tv"])
    iota(T.row3[:, OWN3:], [[-80 * SW, 16], [-80, ROW]], -16 * S, ["row3"])
    iota(T.pos3[:], [[SL, N - 1], [S - C, 2], [1, S]], 2 * C, ["pos3"])
    by_element(T.oA, T.kI[:, :, 8:14], R, ["kI"], "oA")
    place(T.rJ[:], "rJ", LW, OWN1)
    cp("v", T.row1[:].indirect(T.oH[:]), T.val2[:], ["oH", "val2"], ["row1"])
    dma("ys", [(T.lQ[:], T.row1[1:128:16, OWN1:])], ["row1"], ["lQ"])
    dma("ys", [(T.lP[:], T.row1[8:128:16, OWN1:])], ["row1"], ["lP"])
    unpack(4, "B0", 0, R, ["qB0a"])
    window(4, T.wB, WN, 0, R, "wBa")
    dma("ys", [(u8(T.qW[:]), T.wc[:]), (T.sW[:], T.ws[:])], [], ["qW"])
    dma("ys", [(T.val3[0:128:16, :], T.lP[:]), (T.val3[8:128:16, :], T.lQ[:])], ["lP", "lQ"], ["val3"])
    quant("V", 0, 128, T.tv[:], ["tv"], ["qV"])

    mode("1", T.wB, WN, ["wBo%d", "wBa%d"], T.oP1, "oP1", "gC", "tA")
    compose(T.cA, T.tA, T.oA, "A", whole("tA"))
    post(T.cA, "A", "aA")
    quant("A", R, C, T.tA[:], whole("tA"), ["qAo"])
    unpack(0, "A", R, C, ["qAo"])
    window(0, T.wA, WN, R, C, "wAo")

    number(T.lQ[:], "lQ")
    for n in range(2):
        line("sv", T.kU[:, (6 + n) * G + 1:(7 + n) * G], T.lQ[:, h * n:h * n + h], 1.0, float(R + 16 - lo + C * n), ["lQ", "kUg"], ["kUo%d" % n])
    cp("sv", T.l3[:, 0:2, :], T.lP[:], ["lP"], ["l3P"])
    cp("sv", T.l3[:, 2:4, :], T.lQ[:], ["lQ"], ["l3Q"])
    chunked(T.oP2, T.l3[:, 0:2, :], 0.0, ["l3P"], "oP2")
    chunked(T.oK2, T.l3[:, 2:4, :], 0.0, ["l3Q"], "oK2")
    tt(T.kV[:], T.kU[:], T.kM[:], MUL, km + ["kU", "kM3", "kUo0", "kUo1"], ["kV", "kVo"])
    tt(T.kA[:], T.kV[:, 0:4, :], T.kV[:, 4:8, :], ADD, ["kV", "kVo"], ["kA"])
    tt(T.kG[:], T.kA[:, 0:2, 1:G], T.kA[:, 2:4, 1:G], ADD, ["kA"], ["kG"])
    ts(T.kq[:], T.kG[:], 4, None, SHR, None, ["kG"], ["kq"])
    ts(T.kb[:], T.kG[:], float(ROW), float(OWN3 - 1), MUL, ADD, ["kG"], ["kb0", "kb1"])
    ts(T.ka[:], T.kq[:], 1.0 - 16 * ROW, None, MUL, None, ["kq"], ["ka"])
    row_order(T.ka[:], T.kb[:], ["ka", "kb0", "kb1"])
    cp("v", T.row3[:].indirect(T.oT[:]), T.val3[:], ["oT", "val3"], ["row3"])
    r3 = T.row3[:, OWN3:]
    dma("ys", [(T.mK[:], r3[8:128:16, :])], ["row3"], ["mK"])
    dma("ys", [(T.dupe[0:128:32, :], r3[0:128:32, :]), (T.dupe[16:128:32, :], r3[0:128:32, :]),
               (T.dupo[0:128:32, :], r3[16:128:32, :]), (T.dupo[16:128:32, :], r3[16:128:32, :])], ["row3"], ["dup"])
    dma("ys", [(T.mJ[:], r3[3:128:16, :])], ["row3"], ["mJ"])
    dma("ys", [(T.fE[:], T.dupe[0:128:16, :]), (T.fO[:], T.dupo[0:128:16, :])], ["dup"], ["fEO"])
    send_list(block(T.mK), block(T.rK3), "aK3", ["mK"], "rK3")
    place(T.rK3[:], "rK3", ROW, OWN3 + SW)
    cp("v", T.row3[:].indirect(T.oH[:]), T.pos3[:], ["oH", "pos3"], ["row3"])
    dma("ys", [(T.mP[:], r3[3:128:16, :])], ["row3"], ["mP"])
    cp("v", T.oP3[:], T.mP[:, SW:], ["mP"], ["oP3"])
    by_element(T.oB1, T.mJ[:, 0:SW], 0, ["mJ"], "oB1")

    unpack(4, "A", 0, R, ["qAa"])
    window(4, T.wA, WN, 0, R, "wAa")
    gather("gA", T.wA, WN, ["wAo%d", "wAa%d"], T.oP2, "oP2")
    store(0, "A", R, C, ["qAo"])
    cp("v", T.oF[:, 0:SW], T.fE[:, 0:SW], ["fEO"], ["oF0"])
    cp("v", T.oF[:, SW:], T.fO[:, 0:SW], ["fEO"], ["oF1"])
    cp("v", T.qF[:].bitcast(dt.uint32), T.qA[:].bitcast(dt.uint32).indirect(T.oF[:]), ["qAo", "qAa", "oF0", "oF1"], ["qF"])
    cp("sv", T.sF[:], T.sA[:].indirect(T.oF[:]), ["qAo", "qAa", "oF0", "oF1"], ["sF"])
    six = [(t, p) for t in order for p in range(2)]
    e8 = ne // 8
    cut = [eng[e8 * k:e8 * k + e8] for k in range(4)] + [eng[4 * e8:6 * e8], eng[6 * e8:]]
    for x, f in (("q", u8), ("s", lambda a: a)):
        remote([([t], es, f(T[x + "F"][:, R * p + SL * t:R * p + SL * t + SL]), f(T[x + "LF"][:, R * p + SL * (N - 2 - t):R * p + SL * (N - 1 - t)]))
                for (t, p), es in zip(six, cut)], "aF", [x + "F"])
    landed("aF", 2 * got, ["qLF"])
    mm(0, "V", 0, "A", R, C, ["qV", "qAo"])
    cp("sv", T.yt[:, 0:C], bank(0, C), ["ps0"], ["yt0"])
    mode("2", T.wC, N * C, wCk, T.oK2, "oK2", "gA", "tB")
    compose(T.cB1, T.tB, T.oB1, "B1", whole("tB"))
    post(T.cB1, "B1", "aB1")
    quant("B1", R, C, T.tB[:], whole("tB"), ["qB1o"])
    unpack(0, "B1", R, C, ["qB1o"])

    for b in range(4):
        for n in range(2):
            a = W3 * b + C * n
            tt(T.w3[:, a:a + C], bank(b, C), T.gA[:, 2 * b:2 * b + 2, C // 2 * n:C // 2 * (n + 1)], MUL,
               ["ps%d" % b] + ["gA%d%d" % (b, c) for c in range(2)], ["w3%d%d" % (n, b)])
    for b in range(4):
        mm(4 + b, "Ee", 128 * b, "LF", 0, R, ["qEe%d" % b, "qLF"], True, False)
        mm(4 + b, "Eo", 128 * b, "LF", R, R, ["qEo%d" % b, "qLF"], False, True)
    window(4, T.fA, R, 0, R, "fA")
    mm(0, "V", 0, "B1", R, C, ["qV", "qB1o"])
    cp("sv", T.yt[:, C:2 * C], bank(0, C), ["ps0"], ["yt1"])
    unpack(4, "B1", 0, R, ["qB1a"])
    dma("ys", [(T.y[:, 0:2 * C], T.yt[:, 0:2 * C])], ["yt0", "yt1"], [])
    store(C, "B1", R, C, ["qB1o"])
    for b in range(4):
        tt(T.w3[:, W3 * b + 2 * C:W3 * (b + 1)], bank(4 + b, R), T.fA[:, R * b:R * b + R], MUL, ["ps%d" % (4 + b), "fA%d" % b], ["w3a%d" % b])

    def half(b, n, c):
        a, k = CH3[c]
        return T.w3[:, W3 * b + C * n:W3 * (b + 1)].indirect(T.oP3[:, h * n + a // 16:h * n + (a + k) // 16])

    for c, (a, k) in enumerate(CH3):
        for b in range(4):
            slots = ["w3a%d" % b, "oP3"]
            cp("sv", T.g3[:, C * b + a:C * b + a + k], half(b, 0, c), ["w30%d" % b, "w31%d" % b] + slots, ["g3%d%d" % (c, b)])
            tt(T.m3[:, 4 * a + b:4 * (a + k):4], half(b, 1, c), T.g3[:, C * b + a:C * b + a + k], ADD,
               ["w31%d" % b] + slots + ["g3%d%d" % (c, b)], ["M3%d%d" % (c, b)])
        layer("M3", T.m3[:, 4 * a:4 * (a + k)], "tC", c, ["M3%d%d" % (c, b) for b in range(4)], CH3)
    for c, (a, k) in enumerate(CH3):
        quant("C1", a, k, T.tC[:, 4 * a:4 * (a + k)], ["tC%d%d" % (c, b) for b in range(4)], ["qC1%d" % c])
        mm(c, "V", 0, "C1", a, k, ["qV", "qC1%d" % c])
        cp("sv", T.yt[:, 2 * C + a:2 * C + a + k], bank(c, k), ["ps%d" % c], ["yt2%d" % c])
        dma("ys", [(T.y[:, 2 * C + a:2 * C + a + k], T.yt[:, 2 * C + a:2 * C + a + k])], ["yt2%d" % c], [])
        store(2 * C + a, "C1", a, k, ["qC1%d" % c])

    issue()
